import numpy as np, ml_dtypes
CORES = [66,74,82,90,194,202,210,218]
N = 8
import mx_ref
BF = ml_dtypes.bfloat16
def entries(a):
    return np.ascontiguousarray(a.T).reshape(-1)
def table(e):
    return np.ascontiguousarray(np.reshape(e, (-1, 16)).T).astype(np.int32)
def f(rng, *shape):
    return mx_ref.flush((rng.standard_normal(shape, dtype=np.float32) * np.exp2(rng.integers(-2, 3, shape[:-1] + (1,)))).astype(BF))
def wide(rng, *shape, cols=0):
    v = rng.standard_normal(shape, dtype=np.float32) * np.exp2(rng.integers(-12, 13, shape)).astype(np.float32)
    if cols: v *= np.repeat(np.exp2(rng.integers(-cols, cols + 1, shape[:-2] + (1, shape[-1] // 4))) * (rng.random(shape[:-2] + (1, shape[-1] // 4)) > 0.0625), 4, axis=-1).astype(np.float32)
    return mx_ref.flush(v.astype(BF))
T, CAPP, OC, UN = 192, 24, 88, 48
HOST = [0 if c < 128 else 1 for c in CORES]
def term(a, B):
    return np.stack([mx_ref.matmul(mx_ref.quantize(a[:, 512 * i:512 * i + 512]), B) for i in range(4)], axis=2).reshape(128, -1)
def padded(e, k):
    return table(np.concatenate([e, np.full(k - len(e), -1)]))
def lists(rng, fixed=False, blocks=False, plain=False, short=False):
    own = [[[] for d in range(N)] for r in range(N)]
    union = np.full((N, 2, UN), -1)
    for d in range(N):
        half = np.arange(OC) if blocks else rng.permutation(OC)
        ext = [rng.choice(half[(1 - g) * (OC // 2):(2 - g) * (OC // 2)], UN - OC // 2, replace=False) for g in range(2)]
        low = int(rng.integers(0, 2)) if short else -1
        for g in range(2):
            R = [r for r in range(N) if HOST[r] == g]
            mine = list(half[g * (OC // 2):(g + 1) * (OC // 2)]) + list(ext[g])
            p = rng.permutation(len(R)); named = [set() for _ in mine]
            for k in range(CAPP):
                if not fixed: p = rng.permutation(len(R))
                for i in range(len(R) // 2): named[k * (len(R) // 2) + i] = {R[p[2 * i]], R[p[2 * i + 1]]}
            if g == low:
                both = [j for j in range(UN) if j >= OC // 2 or mine[j] in ext[1 - g]]
                for j in both:
                    for r in list(named[j]):
                        to = [t for t in range(OC // 2) if t not in both and r not in named[t]]
                        named[j].remove(r); named[rng.choice(to)].add(r)
            elif not (plain or fixed or short):
                for j in range(OC // 2, UN):
                    for r in list(rng.permutation(list(named[j])))[:rng.integers(0, 3)]:
                        to = [t for t in range(OC // 2) if r not in named[t]]
                        named[j].remove(r); named[rng.choice(to)].add(r)
            at = rng.permutation(UN)
            for j, s in enumerate(named):
                if s: union[d, g, at[j]] = mine[j]
                for r in s: own[r][d].append((mine[j], at[j]))
    send, place, un = [], np.full((N, N, CAPP), -1), []
    for r in range(N):
        send.append(table(rng.permutation(T))); u = []
        for d in range(N):
            o = [own[r][d][i] for i in rng.permutation(CAPP)]
            place[d, r] = [v for v, _ in o]; u += [w for _, w in o]
        un.append(table(u))
    return {"send": np.stack(send), "place": np.stack([table(place[d].reshape(-1)) for d in range(N)]), "un": np.stack(un), "upl": np.stack([padded(union[d].reshape(-1), 96) for d in range(N)])}
def setup_inputs(rng):
    return {"a": f(rng, N, 128, 4 * 512), "b": f(rng, N, 128, 4 * T), **lists(rng)}
def setup_inputs_blocks(rng):
    return {**setup_inputs(rng), **lists(rng, blocks=True, plain=True)}
def setup_inputs_lossless(rng):
    d = setup_inputs(rng)
    a = np.zeros((N, 128, 4 * 128, 4), np.float32)
    for r in range(N):
        k = rng.integers(0, 512, size=4 * 128)
        a[r, k // 4, np.arange(4 * 128), k % 4] = 1.0
    size = 2.0 ** rng.integers(-4, 5, size=(N, OC)); b = rng.integers(-1, 2, size=(N, 128, T, 4)).astype(np.float64)
    for r in range(N):
        s = entries(d["send"][r]).reshape(N, CAPP)
        for o in range(N): b[r][:, s[o]] *= size[o][entries(d["place"][o]).reshape(N, CAPP)[r]][None, :, None]
    d["a"], d["b"] = a.reshape(N, 128, 4 * 512).astype(BF), b.reshape(N, 128, 4 * T).astype(np.float32).astype(BF)
    return d
def setup_inputs_pairs(rng):
    return {**setup_inputs(rng), **lists(rng, fixed=True)}
def setup_inputs_short(rng):
    return {**setup_inputs(rng), **lists(rng, short=True)}
def setup_inputs_spread(rng):
    d = setup_inputs(rng); d["b"] = wide(rng, N, 128, 4 * T); return d
def check_inputs(x):
    b = []
    seen = np.zeros((N, OC), int)
    for r in range(N):
        s, u = entries(x["send"][r]), entries(x["un"][r]).reshape(N, CAPP)
        if sorted(s.tolist()) != list(range(T)): b.append("send")
        if u.min() < 0 or u.max() >= UN: b.append("un")
        for o in range(N):
            p = entries(x["place"][o]).reshape(N, CAPP)[r]
            if p.min() < 0 or p.max() >= OC or len(set(p.tolist())) != CAPP: b.append("place")
            w = entries(x["upl"][o])[:2 * UN].reshape(2, UN)[HOST[r]]
            if (w[u[o]] != p).any(): b.append("upl")
            seen[o][p] += 1
    for o in range(N):
        for g in range(2):
            w = entries(x["upl"][o]); bad = w.min() < -1 or w.max() >= OC or (w[2 * UN:] != -1).any(); w = w[:2 * UN].reshape(2, UN)[g]; w = w[w >= 0]
            if len(set(w.tolist())) != len(w): b.append("upl twice")
    if seen.min() < 2: b.append("a column with fewer than two terms")
    return b
def reference(a, b, send, place, un, upl):
    Z = [term(a[r], mx_ref.quantize(b[r])).reshape(128, T, 4) for r in range(N)]
    y = np.zeros((N, 128, 4 * OC), np.float32)
    for o in range(N):
        parts = []
        for r in range(N):
            t = np.zeros((128, OC, 4), np.float32); t[:, entries(place[o]).reshape(N, CAPP)[r]] = Z[r][:, entries(send[r]).reshape(N, CAPP)[o]]
            parts.append(t.reshape(128, 4 * OC))
        y[o] = mx_ref.total(parts)
    return {"y": y}

@@ -1,0 +1,339 @@
+from concourse.bass import DstId, RemoteDMATransfer
+from concourse.mybir import dt, AluOpType, ActivationFunctionType
+
+N, TCOL, CAPP, OC, UN = 8, 192, 24, 88, 48
+H = 4
+FAR = (H - 1) * UN
+LAND = 512
+OP = 96
+WIN = 56
+
+F32, BF, I32, U16 = "float32", "bfloat16", "int32", "uint16"
+CODE, PLANE = "float8_e4m3fn_x4", "uint8"
+SCRATCH = {
+    "asb": ("sbuf", [128, 2048], BF), "bsb": ("sbuf", [128, 4 * TCOL], BF),
+    "sl": ("sbuf", [128, 12], I32), "ul": ("sbuf", [128, 12], I32), "pl": ("sbuf", [128, 6], I32),
+    "ones": ("sbuf", [128, 516], BF), "cst": ("sbuf", [128, 516], BF),
+    "ipm": ("sbuf", [128, 12], I32), "ek": ("sbuf", [128, 12], I32), "q15": ("sbuf", [128, 12], I32),
+    "ent": ("sbuf", [128, 12], I32), "w1": ("sbuf", [128, 12], I32), "w2": ("sbuf", [128, 12], I32),
+    "dsl": ("sbuf", [128, 12], I32), "x2": ("sbuf", [128, 12], I32),
+    "offs": ("sbuf", [128, 48], U16), "offu": ("sbuf", [128, 48], U16),
+    "bgf": ("sbuf", [128, 384], BF), "bgn": ("sbuf", [128, 384], BF),
+    "bpf": ("sbuf", [128, 8 * FAR], BF), "bpn": ("sbuf", [128, 8 * FAR], BF),
+    "aq": ("sbuf", [128, 512], CODE), "asc": ("sbuf", [128, 512], PLANE),
+    "bfq": ("sbuf", [128, 2 * FAR], CODE), "bfs": ("sbuf", [128, 2 * FAR], PLANE),
+    "bnq": ("sbuf", [128, 2 * FAR], CODE), "bns": ("sbuf", [128, 2 * FAR], PLANE),
+    "hf": ("sbuf", [128, 4 * FAR], BF), "hfq": ("sbuf", [128, FAR], CODE), "hfs": ("sbuf", [128, FAR], PLANE),
+    "hn": ("sbuf", [128, 4 * FAR], BF), "hnq": ("sbuf", [128, FAR], CODE), "hns": ("sbuf", [128, FAR], PLANE),
+    "hg": ("sbuf", [128, 512], BF), "hgq": ("sbuf", [128, 128], CODE), "hgs": ("sbuf", [128, 128], PLANE),
+    "kq": ("sbuf", [128, LAND + 7 * UN], CODE), "ks": ("sbuf", [128, LAND + 7 * UN], PLANE),
+    "mg": ("sbuf", [128, 4 * UN], F32), "xg": ("sbuf", [128, 4 * UN], F32),
+    "mn": ("sbuf", [128, 4 * UN], F32), "xn": ("sbuf", [128, 4 * UN], F32),
+    "val": ("sbuf", [128, 96], F32), "inv": ("sbuf", [128, 288], F32), "rv": ("sbuf", [128, 192], F32),
+    "m16": ("sbuf", [128, 192], F32), "pf": ("sbuf", [128, 2], F32),
+    "lt": ("sbuf", [128, 6], I32), "tr": ("sbuf", [128, 6], I32), "tm": ("sbuf", [128, 6], I32),
+    "p1": ("sbuf", [128, 6], I32), "p2": ("sbuf", [128, 6], I32), "p3": ("sbuf", [128, 6], I32),
+    "p4": ("sbuf", [128, 6], I32), "p5": ("sbuf", [128, 6], I32), "po": ("sbuf", [128, 6], U16),
+    "f0": ("sbuf", [128, 192], F32), "f1": ("sbuf", [128, 96], F32), "f2": ("sbuf", [128, 48], F32),
+    "f3": ("sbuf", [128, 24], F32), "f4": ("sbuf", [128, 12], F32), "offi": ("sbuf", [128, 12], U16),
+    "sn": ("sbuf", [128, 4 * WIN], F32), "sf": ("sbuf", [128, 4 * WIN], F32),
+    "yn": ("sbuf", [128, 4 * OP], F32), "yo": ("sbuf", [128, 4 * OP], F32),
+}
+for _i in range(4):
+    SCRATCH["pa%d" % _i] = ("psum", [128, 512], F32)
+    SCRATCH["pb%d" % _i] = ("psum", [128, 512], F32)
+
+SEMAPHORES = (["sld", "uld", "pld", "bld", "ald0", "ald1", "yst", "lsend", "ones", "gi", "gcst", "gz", "gh", "gv", "gr", "vc",
+               "vq", "vi", "vz", "veq", "voff", "voffn", "vbq", "vbqn", "vbo", "vbno", "vf", "vg", "vhf", "vhn",
+               "vhg", "vinv", "vy", "acg", "acn", "acf", "acfn", "ayn", "arrm"]
+              + [p + str(i) for p in ("vaq", "tf", "tfn", "tg", "tn", "tl", "ag", "an", "am", "vx", "vn") for i in range(4)]
+              + ["arrf%d" % i for i in range(3)] + ["arrn%d" % i for i in range(3)])
+
+
+def slot_of(topo, dst, src):
+    if topo.mates(dst, src):
+        return 0
+    return 1 if topo.same_plane(dst, src) else 2
+
+
+CODE_ENG = {0: (4, 2), 1: (6, 2), 2: (0, 4)}
+PLANE_ENG = {0: (0, 2), 1: (2, 2), 2: (4, 4)}
+
+
+def emask(topo, src, dst, first, count):
+    return sum(1 << e for e in topo.engines(src, dst)[first:first + count])
+
+
+def rank_program(g, core, T, topo):
+    rank = T.rank_of(core)
+    if rank is None:
+        return
+    v, s, te, sy, sem = g.vector, g.scalar, g.tensor, g.sync, T.sem
+    add, mult = AluOpType.add, AluOpType.mult
+    copy = ActivationFunctionType.Copy
+    here = [r for r in range(N) if topo.host(T.cores[r]) == topo.host(core)]
+    there = [r for r in range(N) if topo.host(T.cores[r]) != topo.host(core)]
+    my = here.index(rank)
+    f0, n0 = there[0] * CAPP // 16, here[0] * CAPP // 16
+    peers = [T.cores[here[(my + 1 + j) % H]] for j in range(H - 1)]
+    partner = T.cores[there[my]]
+
+    cnt = {"vc": 0, "vq": 0, "vi": 0, "vz": 0, "vx0": 0, "vx1": 0, "vx2": 0, "vx3": 0}
+
+    def ch(name, ins):
+        ins.then_inc(sem[name], 1)
+        cnt[name] += 1
+
+    def own(name):
+        v.wait_ge(sem[name], cnt[name])
+
+    def fill(out, pattern, base, done):
+        g.iota(out, pattern, base, 0, allow_small_or_imprecise_dtypes=True).then_inc(done, 1)
+
+    for k in range(8):
+        (sy if k < 4 else s).dma_start(T.sl[16 * k:16 * k + 16, :], T.send[:, :]).then_inc(sem.sld, 16)
+    sy.dma_start(T.bsb[:, :], T.b[:, :]).then_inc(sem.bld, 16)
+    for k in range(8):
+        (sy if k < 3 else s).dma_start(T.ul[16 * k:16 * k + 16, :], T.un[:, :]).then_inc(sem.uld, 16)
+    sy.dma_start(T.asb[:, 0:1536], T.a[:, 0:1536]).then_inc(sem.ald0, 16)
+    sy.dma_start(T.asb[:, 1536:2048], T.a[:, 1536:2048]).then_inc(sem.ald1, 16)
+    for k in range(8):
+        sy.dma_start(T.pl[16 * k:16 * k + 16, :], T.upl[:, :]).then_inc(sem.pld, 16)
+
+    g.iota(T.ipm[:, :], [[0, 12]], 0, 1).then_inc(sem.gi, 1)
+    g.iota(T.ek[:, :], [[16, 12]], 0, 0).then_inc(sem.gi, 1)
+    g.wait_ge(sem.ones, 1)
+    g.affine_select(T.cst[:, :], T.ones[:, :], [[1, 516]], AluOpType.is_equal, 0.0, -3, -4).then_inc(sem.gcst, 1)
+    fill(T.bpn[:, :], [[0, 8 * FAR]], 0, sem.gz)
+    fill(T.rv[:, :], [[1, 16], [0, 12]], 0, sem.gr)
+
+    v.memset(T.ones[:, :], 1.0).then_inc(sem.ones, 1)
+    v.wait_ge(sem.gi, 2)
+    ch("vc", v.tensor_scalar(T.q15[:, :], T.ipm[:, :], 15, None, AluOpType.bitwise_and))
+    ch("vq", v.memset(T.bpf[:, 0:768], 0.0))
+    own("vc")
+    ch("vc", v.tensor_tensor(T.ent[:, :], T.q15[:, :], T.ek[:, :], add))
+    ch("vi", v.tensor_copy(T.pf[:, :], T.q15[:, 0:2]))
+    own("vc")
+    ch("vc", v.tensor_scalar(T.w1[:, :], T.ent[:, :], 683, (3 - my) << 14, mult, add))
+    ch("vi", v.tensor_scalar(T.tr[:, 0:3], T.ent[:, 0:3], 13, None, add))
+    ch("vi", v.tensor_scalar(T.tr[:, 3:6], T.ent[:, 3:6], 7, None, add))
+    own("vc")
+    ch("vc", v.tensor_scalar(T.w2[:, :], T.w1[:, :], 14, 3, AluOpType.arith_shift_right, AluOpType.bitwise_and))
+    own("vc")
+    ch("vc", v.tensor_scalar(T.dsl[:, :], T.w2[:, :], UN, None, mult))
+
+    v.wait_ge(sem.sld, 128)
+    for t in range(4):
+        v.tensor_scalar(T.offs[:, 6 * t:6 * t + 6], T.sl[:, f0:f0 + 6], 4, t, mult, add).then_inc(sem.voff, 1)
+    v.wait_ge(sem.uld, 128)
+    own("vc")
+    ch("vc", v.tensor_tensor(T.x2[:, :], T.ul[:, :], T.dsl[:, :], add))
+    for t in range(4):
+        v.tensor_scalar(T.offs[:, 24 + 6 * t:30 + 6 * t], T.sl[:, n0:n0 + 6], 4, t, mult, add).then_inc(sem.voffn, 1)
+    own("vc")
+    for t in range(4):
+        ch("vq", v.tensor_scalar(T.offu[:, 6 * t:6 * t + 6], T.x2[:, f0:f0 + 6], 4, t, mult, add))
+    s.wait_ge(sem.bld, 16)
+    s.wait_ge(sem.voff, 4)
+    s.activation(T.bgf[:, :], T.bsb[:, 0:768].indirect(T.offs[:, 0:24]), copy).then_inc(sem.acg, 1)
+    s.wait_ge(sem.voffn, 4)
+    s.activation(T.bgn[:, :], T.bsb[:, 0:768].indirect(T.offs[:, 24:48]), copy).then_inc(sem.acn, 1)
+    own("vq")
+    v.wait_ge(sem.acg, 1)
+    ch("vq", v.tensor_copy(T.bpf[:, 0:768].indirect(T.offu[:, 0:24]), T.bgf[:, :]))
+
+    def quantise_a(i):
+        v.quantize_mx(T.aq[:, 128 * i:128 * i + 128], T.asc[:, 128 * i:128 * i + 128],
+                      T.asb[:, 512 * i:512 * i + 512]).then_inc(sem["vaq%d" % i], 1)
+
+    v.wait_ge(sem.ald0, 16)
+    quantise_a(0)
+    own("vq")
+    v.quantize_mx(T.bfq[:, 0:FAR], T.bfs[:, 0:FAR], T.bpf[:, 0:4 * FAR]).then_inc(sem.vbq, 1)
+    quantise_a(1)
+    quantise_a(2)
+    v.wait_ge(sem.ald1, 16)
+    quantise_a(3)
+    for t in range(4):
+        ch("vq", v.tensor_scalar(T.offu[:, 24 + 6 * t:30 + 6 * t], T.x2[:, n0:n0 + 6], 4, t, mult, add))
+
+    def product(bank, i, q, p, c0, stop):
+        return te.matmul_mx(T[bank + str(i)][:, 0:FAR], T.aq[:, 128 * i:128 * i + 128], T.asc[:, 128 * i:128 * i + 128],
+                            T[q][:, c0:c0 + FAR], T[p][:, c0:c0 + FAR], True, stop)
+
+    def unpack(bank, t, c0, n, start):
+        return te.matmul_mx(T[bank + str(t)][:, 0:n], T.kq[:, 128 * t:128 * t + 128], T.ks[:, 128 * t:128 * t + 128],
+                            T.kq[:, c0:c0 + n], T.ks[:, c0:c0 + n], start, True)
+
+    te.wait_ge(sem.vbq, 1)
+    for i in range(4):
+        te.wait_ge(sem["vaq%d" % i], 1)
+        product("pa", i, "bfq", "bfs", 0, True).then_inc(sem["tf%d" % i], 1)
+    for i in range(3):
+        s.wait_ge(sem["tf%d" % i], 1)
+        s.activation(T.hf[:, i:4 * FAR:4], T["pa%d" % i][:, 0:FAR], copy).then_inc(sem.acf, 1)
+    v.wait_ge(sem.tf3, 1)
+    v.tensor_copy(T.hf[:, 3:4 * FAR:4], T.pa3[:, 0:FAR]).then_inc(sem.vf, 1)
+    v.wait_ge(sem.acf, 3)
+    v.wait_ge(sem.vf, 1)
+    v.quantize_mx(T.hfq[:, :], T.hfs[:, :], T.hf[:, :]).then_inc(sem.vhf, 1)
+
+    def spread(q, p, at, name):
+        codes, planes = [], []
+        for j, d in enumerate(peers):
+            k = slot_of(topo, d, core)
+            rid, pid = topo.addr(d, core)
+            a, b = at + UN * k, at + UN * (k + 1)
+            codes.append(RemoteDMATransfer(
+                dst_ids=[DstId(rid=rid, pnc=pid)], dma_engine_mask=emask(topo, core, d, *CODE_ENG[k]),
+                remote_sem=sem[name + str(k)], src=T[q][:, UN * j:UN * j + UN].bitcast(dt.uint8),
+                dst=T.kq[:, a:b].bitcast(dt.uint8)))
+            planes.append(RemoteDMATransfer(
+                dst_ids=[DstId(rid=rid, pnc=pid)], dma_engine_mask=emask(topo, core, d, *PLANE_ENG[k]),
+                remote_sem=sem[name + str(k)], src=T[p][:, UN * j:UN * j + UN], dst=T.ks[:, a:b]))
+        g.remote_dma_fused(codes, local_sem=sem.lsend)
+        g.remote_dma_fused(planes, local_sem=sem.lsend)
+
+    g.wait_ge(sem.vhf, 1)
+    spread("hfq", "hfs", LAND, "arrf")
+    fill(T.inv[:, :], [[0, 288]], UN, sem.gv)
+    fill(T.val[:, :], [[0, 2], [1, 48]], 0, sem.gv)
+    fill(T.hg[:, 0:320], [[0, 320]], 0, sem.gh)
+
+    v.wait_ge(sem.acn, 1)
+    v.wait_ge(sem.gz, 1)
+    own("vq")
+    ch("vq", v.tensor_copy(T.bpn[:, 0:768].indirect(T.offu[:, 24:48]), T.bgn[:, :]))
+    ch("vz", v.memset(T.bpf[:, 768:8 * FAR], 0.0))
+    v.wait_ge(sem.pld, 128)
+    ch("vi", v.tensor_scalar(T.p1[:, :], T.pl[:, :], 15, None, AluOpType.bitwise_and))
+    own("vq")
+    v.quantize_mx(T.bnq[:, 0:FAR], T.bns[:, 0:FAR], T.bpn[:, 0:4 * FAR]).then_inc(sem.vbqn, 1)
+    ch("vi", v.tensor_scalar(T.lt[:, :], T.pl[:, :], 0, None, AluOpType.is_lt))
+    ch("vi", v.tensor_scalar(T.p2[:, :], T.pl[:, :], 4, None, AluOpType.arith_shift_right))
+    own("vz")
+    v.quantize_mx(T.bfq[:, FAR:2 * FAR], T.bfs[:, FAR:2 * FAR], T.bpf[:, 4 * FAR:8 * FAR]).then_inc(sem.vbo, 1)
+    own("vi")
+    ch("vi", v.tensor_scalar(T.p3[:, 0:3], T.p1[:, 0:3], 12, None, mult))
+    ch("vi", v.tensor_scalar(T.p3[:, 3:6], T.p1[:, 3:6], 12, 6, mult, add))
+    ch("vi", v.tensor_tensor(T.tm[:, :], T.lt[:, :], T.tr[:, :], mult))
+
+    def constant(t):
+        v.quantize_mx(T.kq[:, 128 * t:128 * t + 128], T.ks[:, 128 * t:128 * t + 128],
+                      T.cst[:, 3 - t:515 - t]).then_inc(sem.veq, 1)
+
+    v.wait_ge(sem.gcst, 1)
+    constant(0)
+    own("vi")
+    ch("vi", v.tensor_tensor(T.p4[:, :], T.p2[:, :], T.p3[:, :], add))
+    constant(1)
+    own("vi")
+    ch("vi", v.tensor_tensor(T.p5[:, :], T.p4[:, :], T.tm[:, :], add))
+    constant(2)
+    own("vi")
+    ch("vi", v.tensor_copy(T.po[:, :], T.p5[:, :]))
+    constant(3)
+    te.wait_ge(sem.vbqn, 1)
+    te.wait_ge(sem.acf, 3)
+    te.wait_ge(sem.vf, 1)
+    for i in range(4):
+        product("pa", i, "bnq", "bns", 0, True).then_inc(sem["tfn%d" % i], 1)
+    te.wait_ge(sem.vbo, 1)
+    for i in range(4):
+        product("pb", i, "bfq", "bfs", FAR, False)
+    for i in range(4):
+        s.wait_ge(sem["tfn%d" % i], 1)
+        s.activation(T.hn[:, i:4 * FAR:4], T["pa%d" % i][:, 0:FAR], copy).then_inc(sem.acfn, 1)
+    v.wait_ge(sem.acfn, 4)
+    v.quantize_mx(T.hnq[:, :], T.hns[:, :], T.hn[:, :]).then_inc(sem.vhn, 1)
+    v.quantize_mx(T.bnq[:, FAR:2 * FAR], T.bns[:, FAR:2 * FAR], T.bpn[:, 4 * FAR:8 * FAR]).then_inc(sem.vbno, 1)
+    g.wait_ge(sem.vhn, 1)
+    spread("hnq", "hns", LAND + 3 * UN, "arrn")
+    v.wait_ge(sem.gv, 2)
+    v.wait_ge(sem.gr, 1)
+    own("vi")
+    ch("vi", v.tensor_copy(T.inv[:, 0:288].indirect(T.po[:, 0:6]), T.val[:, :]))
+    ch("vi", v.tensor_scalar(T.m16[:, :], T.rv[:, :], T.pf[:, 0:1], None, AluOpType.is_equal))
+    own("vi")
+    ch("vi", v.tensor_tensor(T.f0[:, :], T.inv[:, 0:192], T.m16[:, :], mult))
+    own("vi")
+    ch("vi", v.tensor_tensor(T.f1[:, :], T.f0[:, 0:96], T.f0[:, 96:192], add))
+
+    def gather_sum(bank, tsem, asem, mid, part, out, done):
+        def last(t):
+            own("vx%d" % t)
+            v.tensor_tensor(out(t), T[bank + str(t)][:, 2 * UN:FAR], T[part][:, UN * t:UN * t + UN], add).then_inc(done(t), 1)
+
+        for t in range(4):
+            s.wait_ge(sem[tsem + str(t)], 1)
+            s.activation(T[mid][:, UN * t:UN * t + UN], T[bank + str(t)][:, UN:2 * UN], copy).then_inc(sem[asem + str(t)], 1)
+        for t in range(4):
+            v.wait_ge(sem[asem + str(t)], 1)
+            ch("vx%d" % t, v.tensor_tensor(T[part][:, UN * t:UN * t + UN], T[bank + str(t)][:, 0:UN],
+                                           T[mid][:, UN * t:UN * t + UN], add))
+            if t:
+                last(t - 1)
+        last(3)
+
+    te.wait_ge(sem.veq, 4)
+    for k in range(3):
+        te.wait_ge(sem["arrf%d" % k], CODE_ENG[k][1] + PLANE_ENG[k][1])
+    for t in range(4):
+        unpack("pb", t, LAND, FAR, False).then_inc(sem["tg%d" % t], 1)
+    gather_sum("pb", "tg", "ag", "mg", "xg", lambda t: T.hg[:, 320 + t:512:4], lambda t: sem.vg)
+    v.wait_ge(sem.gh, 1)
+    v.wait_ge(sem.vg, 4)
+    v.quantize_mx(T.hgq[:, :], T.hgs[:, :], T.hg[:, :]).then_inc(sem.vhg, 1)
+    rid, pid = topo.addr(partner, core)
+    m8 = emask(topo, core, partner, 0, 8)
+    at = LAND + 6 * UN
+    g.wait_ge(sem.vhg, 1)
+    g.remote_dma(T.kq[:, at:at + UN].bitcast(dt.uint8), T.hgq[:, 80:128].bitcast(dt.uint8), sem.arrm, sem.lsend, pid, rid, m8)
+    g.remote_dma(T.ks[:, at:at + UN], T.hgs[:, 80:128], sem.arrm, sem.lsend, pid, rid, m8)
+
+    own("vi")
+    ch("vi", v.tensor_tensor(T.f2[:, :], T.f1[:, 0:48], T.f1[:, 48:96], add))
+    ch("vz", v.memset(T.sn[:, :], 0.0))
+    own("vi")
+    ch("vi", v.tensor_tensor(T.f3[:, :], T.f2[:, 0:24], T.f2[:, 24:48], add))
+    ch("vz", v.memset(T.sf[:, :], 0.0))
+    own("vi")
+    ch("vi", v.tensor_tensor(T.f4[:, :], T.f3[:, 0:12], T.f3[:, 12:24], add))
+    own("vz")
+    own("vi")
+    v.tensor_copy(T.offi[:, :], T.f4[:, :]).then_inc(sem.vinv, 1)
+
+    te.wait_ge(sem.acfn, 4)
+    te.wait_ge(sem.vbno, 1)
+    for i in range(4):
+        product("pa", i, "bnq", "bns", FAR, False)
+    for k in range(3):
+        te.wait_ge(sem["arrn%d" % k], CODE_ENG[k][1] + PLANE_ENG[k][1])
+    for t in range(4):
+        unpack("pa", t, LAND + FAR, FAR, False).then_inc(sem["tn%d" % t], 1)
+    gather_sum("pa", "tn", "an", "mn", "xn", lambda t: T.sn[:, WIN * t:WIN * t + UN], lambda t: sem["vn%d" % t])
+    gn, gf = 6 * topo.host(core), 6 * topo.host(partner)
+    s.wait_ge(sem.vinv, 1)
+    for t in range(4):
+        s.wait_ge(sem["vn%d" % t], 1)
+        s.activation(T.yn[:, OP * t:OP * t + OP], T.sn[:, WIN * t:WIN * t + WIN].indirect(T.offi[:, gn:gn + 6]),
+                     copy).then_inc(sem.ayn, 1)
+
+    te.wait_ge(sem.arrm, 16)
+    te.wait_ge(sem.vg, 4)
+    for t in range(4):
+        unpack("pb", t, at + UN - 128, 128, True).then_inc(sem["tl%d" % t], 1)
+    for t in range(4):
+        s.wait_ge(sem["tl%d" % t], 1)
+        s.activation(T.sf[:, WIN * t:WIN * t + UN], T["pb%d" % t][:, 80:128], copy).then_inc(sem["am%d" % t], 1)
+    v.wait_ge(sem.vinv, 1)
+    v.wait_ge(sem.ayn, 4)
+    for t in range(4):
+        v.wait_ge(sem["am%d" % t], 1)
+        v.tensor_tensor(T.yo[:, t:4 * OP:4], T.sf[:, WIN * t:WIN * t + WIN].indirect(T.offi[:, gf:gf + 6]),
+                        T.yn[:, OP * t:OP * t + OP], add).then_inc(sem.vy, 1)
+    sy.wait_ge(sem.vy, 4)
+    sy.dma_start(T.y[:, :], T.yo[:, 0:4 * OC]).then_inc(sem.yst, 16)
+    sy.wait_ge(sem.yst, 16)
+    g.wait_ge(sem.lsend, 48)

@@ -3,39 +3,51 @@ from concourse.mybir import dt, AluOpType, ActivationFunctionType
 
 N, TCOL, CAPP, OC, UN = 8, 192, 24, 88, 48
 H = 4
-FAR = (H - 1) * UN
-LAND = 512
+ZW = 208
+ROW = 416
 OP = 96
 WIN = 56
+
+PLAN = [[(0, "f"), (1, "f")], [(2, "fn")], [(0, "n"), (1, "n")]]
+OWN = H - 1
+BLOCKS = [(kind, n) for step in PLAN for n, kinds in step for kind in kinds] + [("n", OWN), ("f", OWN)]
+SLOT = {blk: UN * i for i, blk in enumerate(BLOCKS)}
+FIRST = UN * sum(len(kinds) for n, kinds in PLAN[0])
+K2 = FIRST // 32 * 2
+LEAD = FIRST - 16 * K2
+SENT = UN * (len(BLOCKS) - 2) - FIRST
+REST = 2 * H * UN - 16 * K2
+W1 = max(FIRST, 128)
+STEPS = [[(kind, n) for n, kinds in step for kind in kinds] for step in PLAN]
+LANDS = [("p", 0)] + [blk for step in STEPS[::-1] for blk in step]
+AT = {blk: UN * i for i, blk in enumerate(LANDS)}
+CONST = UN * len(LANDS)
 
 F32, BF, I32, U16 = "float32", "bfloat16", "int32", "uint16"
 CODE, PLANE = "float8_e4m3fn_x4", "uint8"
 SCRATCH = {
     "asb": ("sbuf", [128, 2048], BF), "bsb": ("sbuf", [128, 4 * TCOL], BF),
     "sl": ("sbuf", [128, 12], I32), "ul": ("sbuf", [128, 12], I32), "pl": ("sbuf", [128, 6], I32),
-    "ones": ("sbuf", [128, 516], BF), "cst": ("sbuf", [128, 516], BF),
-    "ipm": ("sbuf", [128, 12], I32), "ek": ("sbuf", [128, 12], I32), "q15": ("sbuf", [128, 12], I32),
-    "ent": ("sbuf", [128, 12], I32), "w1": ("sbuf", [128, 12], I32), "w2": ("sbuf", [128, 12], I32),
-    "dsl": ("sbuf", [128, 12], I32), "x2": ("sbuf", [128, 12], I32),
-    "offs": ("sbuf", [128, 48], U16), "offu": ("sbuf", [128, 48], U16),
-    "bgf": ("sbuf", [128, 384], BF), "bgn": ("sbuf", [128, 384], BF),
-    "bpf": ("sbuf", [128, 8 * FAR], BF), "bpn": ("sbuf", [128, 8 * FAR], BF),
+    "ramp": ("sbuf", [128, 516], BF), "cst": ("sbuf", [128, 516], BF),
+    "ipm": ("sbuf", [128, 2], I32), "ek": ("sbuf", [128, 6], I32), "q15": ("sbuf", [128, 2], I32),
+    "h16": ("sbuf", [128, 2], I32), "h8": ("sbuf", [128, 2], I32), "qf": ("sbuf", [128, 2], F32),
+    "sh": ("sbuf", [128, 2], F32), "up": ("sbuf", [128, 2], F32), "dn": ("sbuf", [128, 2], F32),
+    "tab": ("sbuf", [128, 24], I32), "w1": ("sbuf", [128, 12], I32),
+    "w2": ("sbuf", [128, 12], I32),
+    "base": ("sbuf", [128, 12], I32), "x2": ("sbuf", [128, 12], I32), "g1": ("sbuf", [128, 2], I32),
+    "dump": ("sbuf", [128, 6], I32), "p1": ("sbuf", [128, 6], I32), "p2": ("sbuf", [128, 6], I32),
+    "osd": ("sbuf", [128, 12], U16), "pos": ("sbuf", [128, 12], U16), "po": ("sbuf", [128, 6], U16),
+    "pick": ("sbuf", [128, 2], U16), "lst": ("sbuf", [128, 32], U16), "offi": ("sbuf", [128, 16], U16),
+    "cols": ("sbuf", [128, TCOL], BF), "vals": ("sbuf", [128, TCOL], BF), "val": ("sbuf", [128, 2 * UN], BF),
+    "row": ("sbuf", [128, ROW], BF), "rowt": ("sbuf", [128, ROW], BF),
+    "inv": ("sbuf", [128, ROW], BF), "invt": ("sbuf", [128, 288], BF),
     "aq": ("sbuf", [128, 512], CODE), "asc": ("sbuf", [128, 512], PLANE),
-    "bfq": ("sbuf", [128, 2 * FAR], CODE), "bfs": ("sbuf", [128, 2 * FAR], PLANE),
-    "bnq": ("sbuf", [128, 2 * FAR], CODE), "bns": ("sbuf", [128, 2 * FAR], PLANE),
-    "hf": ("sbuf", [128, 4 * FAR], BF), "hfq": ("sbuf", [128, FAR], CODE), "hfs": ("sbuf", [128, FAR], PLANE),
-    "hn": ("sbuf", [128, 4 * FAR], BF), "hnq": ("sbuf", [128, FAR], CODE), "hns": ("sbuf", [128, FAR], PLANE),
+    "bq": ("sbuf", [128, TCOL], CODE), "bs": ("sbuf", [128, TCOL], PLANE),
+    "zs": ("sbuf", [128, 4 * ZW], BF),
+    "hf": ("sbuf", [128, 4 * W1], BF), "hfq": ("sbuf", [128, W1], CODE), "hfs": ("sbuf", [128, W1], PLANE),
+    "hn": ("sbuf", [128, 4 * REST], BF), "hnq": ("sbuf", [128, max(SENT, 128)], CODE), "hns": ("sbuf", [128, max(SENT, 128)], PLANE),
     "hg": ("sbuf", [128, 512], BF), "hgq": ("sbuf", [128, 128], CODE), "hgs": ("sbuf", [128, 128], PLANE),
-    "kq": ("sbuf", [128, LAND + 7 * UN], CODE), "ks": ("sbuf", [128, LAND + 7 * UN], PLANE),
-    "mg": ("sbuf", [128, 4 * UN], F32), "xg": ("sbuf", [128, 4 * UN], F32),
-    "mn": ("sbuf", [128, 4 * UN], F32), "xn": ("sbuf", [128, 4 * UN], F32),
-    "val": ("sbuf", [128, 96], F32), "inv": ("sbuf", [128, 288], F32), "rv": ("sbuf", [128, 192], F32),
-    "m16": ("sbuf", [128, 192], F32), "pf": ("sbuf", [128, 2], F32),
-    "lt": ("sbuf", [128, 6], I32), "tr": ("sbuf", [128, 6], I32), "tm": ("sbuf", [128, 6], I32),
-    "p1": ("sbuf", [128, 6], I32), "p2": ("sbuf", [128, 6], I32), "p3": ("sbuf", [128, 6], I32),
-    "p4": ("sbuf", [128, 6], I32), "p5": ("sbuf", [128, 6], I32), "po": ("sbuf", [128, 6], U16),
-    "f0": ("sbuf", [128, 192], F32), "f1": ("sbuf", [128, 96], F32), "f2": ("sbuf", [128, 48], F32),
-    "f3": ("sbuf", [128, 24], F32), "f4": ("sbuf", [128, 12], F32), "offi": ("sbuf", [128, 12], U16),
+    "kq": ("sbuf", [128, CONST + 512], CODE), "ks": ("sbuf", [128, CONST + 512], PLANE),
     "sn": ("sbuf", [128, 4 * WIN], F32), "sf": ("sbuf", [128, 4 * WIN], F32),
     "yn": ("sbuf", [128, 4 * OP], F32), "yo": ("sbuf", [128, 4 * OP], F32),
 }
@@ -43,25 +55,24 @@ for _i in range(4):
     SCRATCH["pa%d" % _i] = ("psum", [128, 512], F32)
     SCRATCH["pb%d" % _i] = ("psum", [128, 512], F32)
 
-SEMAPHORES = (["sld", "uld", "pld", "bld", "ald0", "ald1", "yst", "lsend", "ones", "gi", "gcst", "gz", "gh", "gv", "gr", "vc",
-               "vq", "vi", "vz", "veq", "voff", "voffn", "vbq", "vbqn", "vbo", "vbno", "vf", "vg", "vhf", "vhn",
-               "vhg", "vinv", "vy", "acg", "acn", "acf", "acfn", "ayn", "arrm"]
-              + [p + str(i) for p in ("vaq", "tf", "tfn", "tg", "tn", "tl", "ag", "an", "am", "vx", "vn") for i in range(4)]
-              + ["arrf%d" % i for i in range(3)] + ["arrn%d" % i for i in range(3)])
+SEMAPHORES = (["sld", "uld", "pld", "bld", "yst", "lsend", "gi", "gtab", "gcol", "gramp", "gval",
+               "vc", "vq", "vl", "vi", "vz", "vk", "vh", "vr", "veq", "vosd", "vlst", "vbq", "vg", "vhf", "vhn", "vhg", "vinv", "vy",
+               "avals", "ah", "ar", "arrp"]
+              + [p + str(i) for p in ("ald", "vaq", "tz", "az", "tg", "tn", "tl", "am", "vn", "ayn") for i in range(4)]
+              + ["arr%d" % i for i in range(len(PLAN))])
+SHARE = {1: [[(0, 8)], [(0, 8)]], 2: [[(0, 4), (4, 4)], [(0, 4), (4, 4)]], 3: [[(0, 4), (4, 2), (6, 2)], [(4, 4), (0, 2), (2, 2)]]}
 
 
-def slot_of(topo, dst, src):
+def turn(topo, dst, src):
+    if dst == src:
+        return OWN
     if topo.mates(dst, src):
-        return 0
-    return 1 if topo.same_plane(dst, src) else 2
+        return 2
+    return 1 if topo.same_plane(dst, src) else 0
 
 
-CODE_ENG = {0: (4, 2), 1: (6, 2), 2: (0, 4)}
-PLANE_ENG = {0: (0, 2), 1: (2, 2), 2: (4, 4)}
-
-
-def emask(topo, src, dst, first, count):
-    return sum(1 << e for e in topo.engines(src, dst)[first:first + count])
+def side(T, q, p, k, a, n=UN):
+    return T[p][:, a:a + n] if k else T[q][:, a:a + n].bitcast(dt.uint8)
 
 
 def rank_program(g, core, T, topo):
@@ -69,271 +80,255 @@ def rank_program(g, core, T, topo):
     if rank is None:
         return
     v, s, te, sy, sem = g.vector, g.scalar, g.tensor, g.sync, T.sem
-    add, mult = AluOpType.add, AluOpType.mult
+    add, mult, band = AluOpType.add, AluOpType.mult, AluOpType.bitwise_and
     copy = ActivationFunctionType.Copy
     here = [r for r in range(N) if topo.host(T.cores[r]) == topo.host(core)]
     there = [r for r in range(N) if topo.host(T.cores[r]) != topo.host(core)]
-    my = here.index(rank)
-    f0, n0 = there[0] * CAPP // 16, here[0] * CAPP // 16
-    peers = [T.cores[here[(my + 1 + j) % H]] for j in range(H - 1)]
-    partner = T.cores[there[my]]
+    peer = {turn(topo, T.cores[r], core): T.cores[r] for r in here}
+    partner = T.cores[there[here.index(rank)]]
+    block = {r: ("n", turn(topo, T.cores[r], core)) for r in here}
+    block.update({r: ("f", block[q][1]) for r, q in zip(there, here)})
 
-    cnt = {"vc": 0, "vq": 0, "vi": 0, "vz": 0, "vx0": 0, "vx1": 0, "vx2": 0, "vx3": 0}
+    cnt = {}
 
     def ch(name, ins):
         ins.then_inc(sem[name], 1)
-        cnt[name] += 1
+        cnt[name] = cnt.get(name, 0) + 1
 
     def own(name):
         v.wait_ge(sem[name], cnt[name])
 
-    def fill(out, pattern, base, done):
-        g.iota(out, pattern, base, 0, allow_small_or_imprecise_dtypes=True).then_inc(done, 1)
+    def fill(out, pattern, base, done, step=0):
+        g.iota(out, pattern, base, step, allow_small_or_imprecise_dtypes=True).then_inc(done, 1)
 
-    for k in range(8):
-        (sy if k < 4 else s).dma_start(T.sl[16 * k:16 * k + 16, :], T.send[:, :]).then_inc(sem.sld, 16)
+    for k in range(2):
+        s.dma_start(T.sl[16 * k:16 * k + 16, :], T.send[:, :]).then_inc(sem.sld, 16)
+        sy.dma_start(T.ul[16 * k:16 * k + 16, :], T.un[:, :]).then_inc(sem.uld, 16)
     sy.dma_start(T.bsb[:, :], T.b[:, :]).then_inc(sem.bld, 16)
-    for k in range(8):
-        (sy if k < 3 else s).dma_start(T.ul[16 * k:16 * k + 16, :], T.un[:, :]).then_inc(sem.uld, 16)
-    sy.dma_start(T.asb[:, 0:1536], T.a[:, 0:1536]).then_inc(sem.ald0, 16)
-    sy.dma_start(T.asb[:, 1536:2048], T.a[:, 1536:2048]).then_inc(sem.ald1, 16)
-    for k in range(8):
+    for i in range(4):
+        sy.dma_start(T.asb[:, 512 * i:512 * i + 512], T.a[:, 512 * i:512 * i + 512]).then_inc(sem["ald%d" % i], 16)
+    for k in range(2):
         sy.dma_start(T.pl[16 * k:16 * k + 16, :], T.upl[:, :]).then_inc(sem.pld, 16)
+    quarters = [slice(32 * k, 32 * k + 32) for k in range(4)]
 
-    g.iota(T.ipm[:, :], [[0, 12]], 0, 1).then_inc(sem.gi, 1)
-    g.iota(T.ek[:, :], [[16, 12]], 0, 0).then_inc(sem.gi, 1)
-    g.wait_ge(sem.ones, 1)
-    g.affine_select(T.cst[:, :], T.ones[:, :], [[1, 516]], AluOpType.is_equal, 0.0, -3, -4).then_inc(sem.gcst, 1)
-    fill(T.bpn[:, :], [[0, 8 * FAR]], 0, sem.gz)
-    fill(T.rv[:, :], [[1, 16], [0, 12]], 0, sem.gr)
+    g.iota(T.ipm[:, :], [[0, 2]], 0, 1).then_inc(sem.gi, 1)
+    for r in range(0, N, 2):
+        g.iota(T.tab[:, 3 * r:3 * r + 6], [[SLOT[block[r + 1]] - SLOT[block[r]], 2], [0, 3]], SLOT[block[r]], 0).then_inc(sem.gtab, 1)
+    fill(T.cols[:, :], [[1, TCOL]], 0, sem.gcol)
+    fill(T.ramp[:, :], [[1, 516]], -3, sem.gramp, -4)
+    fill(T.val[:, :], [[0, 2], [1, UN]], 0, sem.gval)
+    g.iota(T.ek[:, :], [[16, 6]], 208, 0).then_inc(sem.gval, 1)
 
-    v.memset(T.ones[:, :], 1.0).then_inc(sem.ones, 1)
-    v.wait_ge(sem.gi, 2)
-    ch("vc", v.tensor_scalar(T.q15[:, :], T.ipm[:, :], 15, None, AluOpType.bitwise_and))
-    ch("vq", v.memset(T.bpf[:, 0:768], 0.0))
+    ch("vl", v.memset(T.row[:, :], float(TCOL)))
+    ch("vz", v.memset(T.zs[:, TCOL:4 * ZW:ZW], 0.0))
+    v.wait_ge(sem.gi, 1)
+    ch("vc", v.tensor_scalar(T.h16[:, :], T.ipm[:, :], 16, None, band))
+    ch("vc", v.tensor_scalar(T.h8[:, :], T.ipm[:, :], 8, None, band))
+    ch("vq", v.tensor_scalar(T.q15[:, :], T.ipm[:, :], 15, None, band))
+    if FIRST < W1:
+        ch("vh", v.memset(T.hf[:, 4 * FIRST:4 * W1], 0.0))
     own("vc")
-    ch("vc", v.tensor_tensor(T.ent[:, :], T.q15[:, :], T.ek[:, :], add))
-    ch("vi", v.tensor_copy(T.pf[:, :], T.q15[:, 0:2]))
-    own("vc")
-    ch("vc", v.tensor_scalar(T.w1[:, :], T.ent[:, :], 683, (3 - my) << 14, mult, add))
-    ch("vi", v.tensor_scalar(T.tr[:, 0:3], T.ent[:, 0:3], 13, None, add))
-    ch("vi", v.tensor_scalar(T.tr[:, 3:6], T.ent[:, 3:6], 7, None, add))
-    own("vc")
-    ch("vc", v.tensor_scalar(T.w2[:, :], T.w1[:, :], 14, 3, AluOpType.arith_shift_right, AluOpType.bitwise_and))
-    own("vc")
-    ch("vc", v.tensor_scalar(T.dsl[:, :], T.w2[:, :], UN, None, mult))
-
-    v.wait_ge(sem.sld, 128)
-    for t in range(4):
-        v.tensor_scalar(T.offs[:, 6 * t:6 * t + 6], T.sl[:, f0:f0 + 6], 4, t, mult, add).then_inc(sem.voff, 1)
-    v.wait_ge(sem.uld, 128)
-    own("vc")
-    ch("vc", v.tensor_tensor(T.x2[:, :], T.ul[:, :], T.dsl[:, :], add))
-    for t in range(4):
-        v.tensor_scalar(T.offs[:, 24 + 6 * t:30 + 6 * t], T.sl[:, n0:n0 + 6], 4, t, mult, add).then_inc(sem.voffn, 1)
-    own("vc")
-    for t in range(4):
-        ch("vq", v.tensor_scalar(T.offu[:, 6 * t:6 * t + 6], T.x2[:, f0:f0 + 6], 4, t, mult, add))
-    s.wait_ge(sem.bld, 16)
-    s.wait_ge(sem.voff, 4)
-    s.activation(T.bgf[:, :], T.bsb[:, 0:768].indirect(T.offs[:, 0:24]), copy).then_inc(sem.acg, 1)
-    s.wait_ge(sem.voffn, 4)
-    s.activation(T.bgn[:, :], T.bsb[:, 0:768].indirect(T.offs[:, 24:48]), copy).then_inc(sem.acn, 1)
+    ch("vc", v.tensor_scalar(T.sh[:, :], T.h16[:, :], -1, 16, mult, add))
+    ch("vc", v.tensor_scalar(T.up[:, :], T.h8[:, :], -0.125, 1, mult, add))
+    ch("vc", v.tensor_scalar(T.dn[:, :], T.h8[:, :], 0.125, None, mult))
     own("vq")
-    v.wait_ge(sem.acg, 1)
-    ch("vq", v.tensor_copy(T.bpf[:, 0:768].indirect(T.offu[:, 0:24]), T.bgf[:, :]))
+    ch("vi", v.tensor_copy(T.qf[:, :], T.q15[:, :]))
+    own("vc")
+    v.wait_ge(sem.gtab, 4)
+    ch("vc", v.tensor_scalar(T.w1[0:32, :], T.tab[0:32, 0:24:2], T.up[0:32, 0:1], T.sh[0:32, 0:1], mult, add))
+    ch("vc", v.tensor_scalar(T.w2[0:32, :], T.tab[0:32, 1:24:2], T.dn[0:32, 0:1], None, mult))
+    ch("vq", v.tensor_scalar(T.g1[:, :], T.q15[:, :], 16, T.sh[:, 0:1], mult, add))
 
     def quantise_a(i):
+        v.wait_ge(sem["ald%d" % i], 16)
         v.quantize_mx(T.aq[:, 128 * i:128 * i + 128], T.asc[:, 128 * i:128 * i + 128],
                       T.asb[:, 512 * i:512 * i + 512]).then_inc(sem["vaq%d" % i], 1)
 
-    v.wait_ge(sem.ald0, 16)
-    quantise_a(0)
+    v.wait_ge(sem.sld, 32)
+    for q in quarters:
+        v.tensor_copy(T.osd[q, :], T.sl[0:32, :]).then_inc(sem.vosd, 1)
+    s.wait_ge(sem.gcol, 1)
+    s.wait_ge(sem.vosd, 4)
+    s.activation(T.vals[:, :], T.cols[:, :].indirect(T.osd[:, :]), copy).then_inc(sem.avals, 1)
+    own("vc")
+    ch("vc", v.tensor_tensor(T.base[0:32, :], T.w1[0:32, :], T.w2[0:32, :], add))
     own("vq")
-    v.quantize_mx(T.bfq[:, 0:FAR], T.bfs[:, 0:FAR], T.bpf[:, 0:4 * FAR]).then_inc(sem.vbq, 1)
+    ch("vl", v.tensor_copy(T.pick[:, 0:1], T.g1[:, 0:1]))
+    ch("vl", v.tensor_scalar(T.pick[:, 1:2], T.g1[:, 1:2], 256, 400, add, AluOpType.min))
+    v.wait_ge(sem.uld, 32)
+    own("vc")
+    ch("vc", v.tensor_tensor(T.x2[0:32, :], T.ul[0:32, :], T.base[0:32, :], add))
+    v.wait_ge(sem.bld, 16)
+    v.quantize_mx(T.bq[:, :], T.bs[:, :], T.bsb[:, :]).then_inc(sem.vbq, 1)
+    own("vc")
+    for q in quarters:
+        ch("vl", v.tensor_copy(T.pos[q, :], T.x2[0:32, :]))
+    quantise_a(0)
+    own("vl")
+    v.wait_ge(sem.avals, 1)
+    ch("vl", v.tensor_copy(T.row[:, :].indirect(T.pos[:, :]), T.vals[:, :]))
     quantise_a(1)
+    own("vl")
+    ch("vl", v.transpose(T.rowt[:, :], T.row[:, :]))
     quantise_a(2)
-    v.wait_ge(sem.ald1, 16)
+    own("vl")
+    v.tensor_copy(T.lst[:, :], T.rowt[:, :].indirect(T.pick[:, :])).then_inc(sem.vlst, 1)
     quantise_a(3)
-    for t in range(4):
-        ch("vq", v.tensor_scalar(T.offu[:, 24 + 6 * t:30 + 6 * t], T.x2[:, n0:n0 + 6], 4, t, mult, add))
-
-    def product(bank, i, q, p, c0, stop):
-        return te.matmul_mx(T[bank + str(i)][:, 0:FAR], T.aq[:, 128 * i:128 * i + 128], T.asc[:, 128 * i:128 * i + 128],
-                            T[q][:, c0:c0 + FAR], T[p][:, c0:c0 + FAR], True, stop)
-
-    def unpack(bank, t, c0, n, start):
-        return te.matmul_mx(T[bank + str(t)][:, 0:n], T.kq[:, 128 * t:128 * t + 128], T.ks[:, 128 * t:128 * t + 128],
-                            T.kq[:, c0:c0 + n], T.ks[:, c0:c0 + n], start, True)
 
     te.wait_ge(sem.vbq, 1)
     for i in range(4):
         te.wait_ge(sem["vaq%d" % i], 1)
-        product("pa", i, "bfq", "bfs", 0, True).then_inc(sem["tf%d" % i], 1)
-    for i in range(3):
-        s.wait_ge(sem["tf%d" % i], 1)
-        s.activation(T.hf[:, i:4 * FAR:4], T["pa%d" % i][:, 0:FAR], copy).then_inc(sem.acf, 1)
-    v.wait_ge(sem.tf3, 1)
-    v.tensor_copy(T.hf[:, 3:4 * FAR:4], T.pa3[:, 0:FAR]).then_inc(sem.vf, 1)
-    v.wait_ge(sem.acf, 3)
-    v.wait_ge(sem.vf, 1)
-    v.quantize_mx(T.hfq[:, :], T.hfs[:, :], T.hf[:, :]).then_inc(sem.vhf, 1)
+        te.matmul_mx(T["pa%d" % i][:, 0:TCOL], T.aq[:, 128 * i:128 * i + 128], T.asc[:, 128 * i:128 * i + 128],
+                     T.bq[:, :], T.bs[:, :], True, True).then_inc(sem["tz%d" % i], 1)
 
-    def spread(q, p, at, name):
-        codes, planes = [], []
-        for j, d in enumerate(peers):
-            k = slot_of(topo, d, core)
-            rid, pid = topo.addr(d, core)
-            a, b = at + UN * k, at + UN * (k + 1)
-            codes.append(RemoteDMATransfer(
-                dst_ids=[DstId(rid=rid, pnc=pid)], dma_engine_mask=emask(topo, core, d, *CODE_ENG[k]),
-                remote_sem=sem[name + str(k)], src=T[q][:, UN * j:UN * j + UN].bitcast(dt.uint8),
-                dst=T.kq[:, a:b].bitcast(dt.uint8)))
-            planes.append(RemoteDMATransfer(
-                dst_ids=[DstId(rid=rid, pnc=pid)], dma_engine_mask=emask(topo, core, d, *PLANE_ENG[k]),
-                remote_sem=sem[name + str(k)], src=T[p][:, UN * j:UN * j + UN], dst=T.ks[:, a:b]))
-        g.remote_dma_fused(codes, local_sem=sem.lsend)
-        g.remote_dma_fused(planes, local_sem=sem.lsend)
+    def leave(i):
+        s.wait_ge(sem["tz%d" % i], 1)
+        s.activation(T.zs[:, ZW * i:ZW * i + TCOL], T["pa%d" % i][:, 0:TCOL], copy).then_inc(sem["az%d" % i], 1)
 
-    g.wait_ge(sem.vhf, 1)
-    spread("hfq", "hfs", LAND, "arrf")
-    fill(T.inv[:, :], [[0, 288]], UN, sem.gv)
-    fill(T.val[:, :], [[0, 2], [1, 48]], 0, sem.gv)
-    fill(T.hg[:, 0:320], [[0, 320]], 0, sem.gh)
+    def first(i):
+        return T.hf[:, i:4 * FIRST:4], T.zs[:, ZW * i:ZW * i + TCOL + 1].indirect(T.lst[:, 0:FIRST // 16])
 
-    v.wait_ge(sem.acn, 1)
-    v.wait_ge(sem.gz, 1)
-    own("vq")
-    ch("vq", v.tensor_copy(T.bpn[:, 0:768].indirect(T.offu[:, 24:48]), T.bgn[:, :]))
-    ch("vz", v.memset(T.bpf[:, 768:8 * FAR], 0.0))
-    v.wait_ge(sem.pld, 128)
-    ch("vi", v.tensor_scalar(T.p1[:, :], T.pl[:, :], 15, None, AluOpType.bitwise_and))
-    own("vq")
-    v.quantize_mx(T.bnq[:, 0:FAR], T.bns[:, 0:FAR], T.bpn[:, 0:4 * FAR]).then_inc(sem.vbqn, 1)
-    ch("vi", v.tensor_scalar(T.lt[:, :], T.pl[:, :], 0, None, AluOpType.is_lt))
-    ch("vi", v.tensor_scalar(T.p2[:, :], T.pl[:, :], 4, None, AluOpType.arith_shift_right))
+    def rest(i):
+        return T.hn[:, i:4 * REST:4], T.zs[:, ZW * i:ZW * i + TCOL + 1].indirect(T.lst[:, K2:24])
+
+    def on_scalar(pair, done):
+        s.activation(pair[0], pair[1], copy).then_inc(done, 1)
+
+    for i in range(4):
+        leave(i)
+    s.wait_ge(sem.vlst, 1)
+    s.wait_ge(sem.vz, 1)
+    s.wait_ge(sem.az0, 1)
+    s.wait_ge(sem.az1, 1)
+    on_scalar(rest(0), sem.ar)
+    on_scalar(rest(1), sem.ar)
+
+    v.wait_ge(sem.vlst, 1)
     own("vz")
-    v.quantize_mx(T.bfq[:, FAR:2 * FAR], T.bfs[:, FAR:2 * FAR], T.bpf[:, 4 * FAR:8 * FAR]).then_inc(sem.vbo, 1)
-    own("vi")
-    ch("vi", v.tensor_scalar(T.p3[:, 0:3], T.p1[:, 0:3], 12, None, mult))
-    ch("vi", v.tensor_scalar(T.p3[:, 3:6], T.p1[:, 3:6], 12, 6, mult, add))
-    ch("vi", v.tensor_tensor(T.tm[:, :], T.lt[:, :], T.tr[:, :], mult))
+    for i in range(4):
+        v.wait_ge(sem["az%d" % i], 1)
+        ch("vh", v.tensor_copy(*first(i)))
+    own("vh")
+    v.quantize_mx(T.hfq[:, :], T.hfs[:, :], T.hf[:, :]).then_inc(sem.vhf, 1)
+    ch("vr", v.tensor_copy(*rest(2)))
+    ch("vr", v.tensor_copy(*rest(3)))
+    v.wait_ge(sem.gramp, 1)
+    ch("vk", v.tensor_scalar(T.cst[:, :], T.ramp[:, :], 0, None, AluOpType.is_equal))
+    v.wait_ge(sem.ar, 2)
+    own("vr")
+    if SENT:
+        v.quantize_mx(T.hnq[:, :], T.hns[:, :], T.hn[:, 4 * LEAD:4 * (LEAD + SENT)]).then_inc(sem.vhn, 1)
+
+    sent = 16
+    for i, step in enumerate(PLAN):
+        if i < 2:
+            g.wait_ge(sem.vhn if i else sem.vhf, 1)
+        for k in range(2):
+            call = []
+            for j, (n, kinds) in enumerate(step):
+                blk, width, d = (kinds[0], n), UN * len(kinds), peer[n]
+                rid, pid = topo.addr(d, core)
+                e0, count = SHARE[len(step)][k][j]
+                src = side(T, "hnq", "hns", k, SLOT[blk] - FIRST, width) if i else side(T, "hfq", "hfs", k, SLOT[blk], width)
+                call.append(RemoteDMATransfer(
+                    dst_ids=[DstId(rid=rid, pnc=pid)], dma_engine_mask=sum(1 << e for e in topo.engines(core, d)[e0:e0 + count]),
+                    remote_sem=sem["arr%d" % i], src=src, dst=side(T, "kq", "ks", k, AT[blk], width)))
+            g.remote_dma_fused(call, local_sem=sem.lsend)
+            sent += 8
 
     def constant(t):
-        v.quantize_mx(T.kq[:, 128 * t:128 * t + 128], T.ks[:, 128 * t:128 * t + 128],
-                      T.cst[:, 3 - t:515 - t]).then_inc(sem.veq, 1)
+        a = CONST + 128 * t
+        v.quantize_mx(T.kq[:, a:a + 128], T.ks[:, a:a + 128], T.cst[:, 3 - t:515 - t]).then_inc(sem.veq, 1)
 
-    v.wait_ge(sem.gcst, 1)
+    own("vk")
+    v.wait_ge(sem.pld, 32)
+    v.wait_ge(sem.gval, 2)
+    own("vi")
+    for q in quarters:
+        ch("vi", v.tensor_scalar(T.p1[q, :], T.pl[0:32, :], 511, None, band))
+    ch("vi", v.tensor_scalar(T.dump[:, :], T.ek[:, :], T.qf[:, 0:1], None, add))
+    ch("vi", v.memset(T.inv[:, :], float(UN)))
     constant(0)
     own("vi")
-    ch("vi", v.tensor_tensor(T.p4[:, :], T.p2[:, :], T.p3[:, :], add))
+    ch("vi", v.tensor_tensor(T.p2[:, :], T.p1[:, :], T.dump[:, :], AluOpType.min))
     constant(1)
     own("vi")
-    ch("vi", v.tensor_tensor(T.p5[:, :], T.p4[:, :], T.tm[:, :], add))
+    for h in range(2):
+        ch("vi", v.tensor_scalar(T.po[:, 3 * h:3 * h + 3], T.p2[:, 3 * h:3 * h + 3], T.sh[:, 0:1], OP * h, add, add))
     constant(2)
-    own("vi")
-    ch("vi", v.tensor_copy(T.po[:, :], T.p5[:, :]))
     constant(3)
-    te.wait_ge(sem.vbqn, 1)
-    te.wait_ge(sem.acf, 3)
-    te.wait_ge(sem.vf, 1)
-    for i in range(4):
-        product("pa", i, "bnq", "bns", 0, True).then_inc(sem["tfn%d" % i], 1)
-    te.wait_ge(sem.vbo, 1)
-    for i in range(4):
-        product("pb", i, "bfq", "bfs", FAR, False)
-    for i in range(4):
-        s.wait_ge(sem["tfn%d" % i], 1)
-        s.activation(T.hn[:, i:4 * FAR:4], T["pa%d" % i][:, 0:FAR], copy).then_inc(sem.acfn, 1)
-    v.wait_ge(sem.acfn, 4)
-    v.quantize_mx(T.hnq[:, :], T.hns[:, :], T.hn[:, :]).then_inc(sem.vhn, 1)
-    v.quantize_mx(T.bnq[:, FAR:2 * FAR], T.bns[:, FAR:2 * FAR], T.bpn[:, 4 * FAR:8 * FAR]).then_inc(sem.vbno, 1)
-    g.wait_ge(sem.vhn, 1)
-    spread("hnq", "hns", LAND + 3 * UN, "arrn")
-    v.wait_ge(sem.gv, 2)
-    v.wait_ge(sem.gr, 1)
     own("vi")
-    ch("vi", v.tensor_copy(T.inv[:, 0:288].indirect(T.po[:, 0:6]), T.val[:, :]))
-    ch("vi", v.tensor_scalar(T.m16[:, :], T.rv[:, :], T.pf[:, 0:1], None, AluOpType.is_equal))
+    ch("vi", v.tensor_copy(T.inv[:, :].indirect(T.po[:, :]), T.val[:, :]))
+    ch("vg", v.memset(T.hg[:, 0:320], 0.0))
     own("vi")
-    ch("vi", v.tensor_tensor(T.f0[:, :], T.inv[:, 0:192], T.m16[:, :], mult))
+    ch("vi", v.transpose(T.invt[:, :], T.inv[:, 0:288]))
+    ch("vz", v.memset(T.sn[:, UN:4 * WIN:WIN], 0.0))
+    ch("vz", v.memset(T.sf[:, UN:4 * WIN:WIN], 0.0))
     own("vi")
-    ch("vi", v.tensor_tensor(T.f1[:, :], T.f0[:, 0:96], T.f0[:, 96:192], add))
+    own("vz")
+    v.tensor_copy(T.offi[:, :], T.invt[:, :].indirect(T.pick[:, 0:1])).then_inc(sem.vinv, 1)
 
-    def gather_sum(bank, tsem, asem, mid, part, out, done):
-        def last(t):
-            own("vx%d" % t)
-            v.tensor_tensor(out(t), T[bank + str(t)][:, 2 * UN:FAR], T[part][:, UN * t:UN * t + UN], add).then_inc(done(t), 1)
+    def unpack(bank, t, blk, start, stop):
+        a, c = CONST + 128 * t, AT[blk]
+        return te.matmul_mx(T[bank + str(t)][:, 0:128], T.kq[:, a:a + 128], T.ks[:, a:a + 128],
+                            T.kq[:, c:c + 128], T.ks[:, c:c + 128], start, stop)
 
-        for t in range(4):
-            s.wait_ge(sem[tsem + str(t)], 1)
-            s.activation(T[mid][:, UN * t:UN * t + UN], T[bank + str(t)][:, UN:2 * UN], copy).then_inc(sem[asem + str(t)], 1)
-        for t in range(4):
-            v.wait_ge(sem[asem + str(t)], 1)
-            ch("vx%d" % t, v.tensor_tensor(T[part][:, UN * t:UN * t + UN], T[bank + str(t)][:, 0:UN],
-                                           T[mid][:, UN * t:UN * t + UN], add))
-            if t:
-                last(t - 1)
-        last(3)
+    def add_up(kind, bank, done):
+        seen = 0
+        for i, step in enumerate(STEPS):
+            landed = [blk for blk in step if blk[0] == kind]
+            te.wait_ge(sem["arr%d" % i], 16)
+            for t in range(4):
+                for j, blk in enumerate(landed):
+                    ins = unpack(bank, t, blk, seen + j == 0, seen + j == 2)
+                    if seen + j == 2:
+                        ins.then_inc(sem[done + str(t)], 1)
+            seen += len(landed)
+            if seen == 3:
+                return
+
+    def mine(kind, t):
+        a = 4 * (SLOT[kind, OWN] - 16 * K2)
+        return T.hn[:, a + t:a + 4 * UN:4]
 
     te.wait_ge(sem.veq, 4)
-    for k in range(3):
-        te.wait_ge(sem["arrf%d" % k], CODE_ENG[k][1] + PLANE_ENG[k][1])
+    add_up("f", "pb", "tg")
     for t in range(4):
-        unpack("pb", t, LAND, FAR, False).then_inc(sem["tg%d" % t], 1)
-    gather_sum("pb", "tg", "ag", "mg", "xg", lambda t: T.hg[:, 320 + t:512:4], lambda t: sem.vg)
-    v.wait_ge(sem.gh, 1)
-    v.wait_ge(sem.vg, 4)
+        v.wait_ge(sem["tg%d" % t], 1)
+        ch("vg", v.tensor_tensor(T.hg[:, 320 + t:512:4], T["pb%d" % t][:, 0:UN], mine("f", t), add))
+    own("vg")
     v.quantize_mx(T.hgq[:, :], T.hgs[:, :], T.hg[:, :]).then_inc(sem.vhg, 1)
     rid, pid = topo.addr(partner, core)
-    m8 = emask(topo, core, partner, 0, 8)
-    at = LAND + 6 * UN
     g.wait_ge(sem.vhg, 1)
-    g.remote_dma(T.kq[:, at:at + UN].bitcast(dt.uint8), T.hgq[:, 80:128].bitcast(dt.uint8), sem.arrm, sem.lsend, pid, rid, m8)
-    g.remote_dma(T.ks[:, at:at + UN], T.hgs[:, 80:128], sem.arrm, sem.lsend, pid, rid, m8)
+    for k in range(2):
+        g.remote_dma(side(T, "kq", "ks", k, AT["p", 0]), side(T, "hgq", "hgs", k, 128 - UN), sem.arrp, sem.lsend,
+                     pid, rid, topo.mask(core, partner))
 
-    own("vi")
-    ch("vi", v.tensor_tensor(T.f2[:, :], T.f1[:, 0:48], T.f1[:, 48:96], add))
-    ch("vz", v.memset(T.sn[:, :], 0.0))
-    own("vi")
-    ch("vi", v.tensor_tensor(T.f3[:, :], T.f2[:, 0:24], T.f2[:, 24:48], add))
-    ch("vz", v.memset(T.sf[:, :], 0.0))
-    own("vi")
-    ch("vi", v.tensor_tensor(T.f4[:, :], T.f3[:, 0:12], T.f3[:, 12:24], add))
-    own("vz")
-    own("vi")
-    v.tensor_copy(T.offi[:, :], T.f4[:, :]).then_inc(sem.vinv, 1)
-
-    te.wait_ge(sem.acfn, 4)
-    te.wait_ge(sem.vbno, 1)
     for i in range(4):
-        product("pa", i, "bnq", "bns", FAR, False)
-    for k in range(3):
-        te.wait_ge(sem["arrn%d" % k], CODE_ENG[k][1] + PLANE_ENG[k][1])
-    for t in range(4):
-        unpack("pa", t, LAND + FAR, FAR, False).then_inc(sem["tn%d" % t], 1)
-    gather_sum("pa", "tn", "an", "mn", "xn", lambda t: T.sn[:, WIN * t:WIN * t + UN], lambda t: sem["vn%d" % t])
+        te.wait_ge(sem["az%d" % i], 1)
+    add_up("n", "pa", "tn")
     gn, gf = 6 * topo.host(core), 6 * topo.host(partner)
     s.wait_ge(sem.vinv, 1)
     for t in range(4):
+        v.wait_ge(sem["tn%d" % t], 1)
+        v.tensor_tensor(T.sn[:, WIN * t:WIN * t + UN], T["pa%d" % t][:, 0:UN], mine("n", t), add).then_inc(sem["vn%d" % t], 1)
         s.wait_ge(sem["vn%d" % t], 1)
-        s.activation(T.yn[:, OP * t:OP * t + OP], T.sn[:, WIN * t:WIN * t + WIN].indirect(T.offi[:, gn:gn + 6]),
-                     copy).then_inc(sem.ayn, 1)
+        s.activation(T.yn[:, OP * t:OP * t + OP], T.sn[:, WIN * t:WIN * t + UN + 1].indirect(T.offi[:, gn:gn + 6]),
+                     copy).then_inc(sem["ayn%d" % t], 1)
 
-    te.wait_ge(sem.arrm, 16)
-    te.wait_ge(sem.vg, 4)
+    te.wait_ge(sem.arrp, 16)
+    te.wait_ge(sem.vg, cnt["vg"])
     for t in range(4):
-        unpack("pb", t, at + UN - 128, 128, True).then_inc(sem["tl%d" % t], 1)
-    for t in range(4):
+        unpack("pb", t, ("p", 0), True, True).then_inc(sem["tl%d" % t], 1)
         s.wait_ge(sem["tl%d" % t], 1)
-        s.activation(T.sf[:, WIN * t:WIN * t + UN], T["pb%d" % t][:, 80:128], copy).then_inc(sem["am%d" % t], 1)
+        s.activation(T.sf[:, WIN * t:WIN * t + UN], T["pb%d" % t][:, 0:UN], copy).then_inc(sem["am%d" % t], 1)
     v.wait_ge(sem.vinv, 1)
-    v.wait_ge(sem.ayn, 4)
     for t in range(4):
+        v.wait_ge(sem["ayn%d" % t], 1)
         v.wait_ge(sem["am%d" % t], 1)
-        v.tensor_tensor(T.yo[:, t:4 * OP:4], T.sf[:, WIN * t:WIN * t + WIN].indirect(T.offi[:, gf:gf + 6]),
+        v.tensor_tensor(T.yo[:, t:4 * OP:4], T.sf[:, WIN * t:WIN * t + UN + 1].indirect(T.offi[:, gf:gf + 6]),
                         T.yn[:, OP * t:OP * t + OP], add).then_inc(sem.vy, 1)
     sy.wait_ge(sem.vy, 4)
     sy.dma_start(T.y[:, :], T.yo[:, 0:4 * OC]).then_inc(sem.yst, 16)
     sy.wait_ge(sem.yst, 16)
-    g.wait_ge(sem.lsend, 48)
+    g.wait_ge(sem.lsend, sent)

@@ -8,20 +8,25 @@ ROW = 416
 OP = 96
 WIN = 56
 
-PLAN = [[(0, "f"), (1, "f")], [(2, "fn")], [(0, "n"), (1, "n")]]
+PLAN = [[(0, "f")], [(1, "fn")], [(2, "fn")], [(0, "n")]]
 OWN = H - 1
 BLOCKS = [(kind, n) for step in PLAN for n, kinds in step for kind in kinds] + [("n", OWN), ("f", OWN)]
 SLOT = {blk: UN * i for i, blk in enumerate(BLOCKS)}
-FIRST = UN * sum(len(kinds) for n, kinds in PLAN[0])
-K2 = FIRST // 32 * 2
-LEAD = FIRST - 16 * K2
-SENT = UN * (len(BLOCKS) - 2) - FIRST
-REST = 2 * H * UN - 16 * K2
-W1 = max(FIRST, 128)
+SPLIT = 1
+TILE = [0, 1, 2, 2]
+FROM = [SLOT[PLAN[TILE.index(j)][0][1][0], PLAN[TILE.index(j)][0][0]] for j in range(max(TILE) + 1)] + [SLOT["n", OWN]]
+SIZE = [b - a for a, b in zip(FROM, FROM[1:])]
+LEAD = [a % 32 for a in FROM]
+K3 = SLOT["n", OWN] // 16
+YW = UN + OP
+ON_VECTOR = "00 01 03 q0 12 13 cst q1 23 zero q2".split()
+ON_SCALAR = "02 10 11 20 21 22".split()
 STEPS = [[(kind, n) for n, kinds in step for kind in kinds] for step in PLAN]
 LANDS = [("p", 0)] + [blk for step in STEPS[::-1] for blk in step]
 AT = {blk: UN * i for i, blk in enumerate(LANDS)}
-CONST = UN * len(LANDS)
+CONST = UN * len(LANDS) + 128
+
+ORDER = "g s0 base s1 un pick pos b a0 row a1 a2 turn a3 list".split()
 
 F32, BF, I32, U16 = "float32", "bfloat16", "int32", "uint16"
 CODE, PLANE = "float8_e4m3fn_x4", "uint8"
@@ -44,22 +49,25 @@ SCRATCH = {
     "aq": ("sbuf", [128, 512], CODE), "asc": ("sbuf", [128, 512], PLANE),
     "bq": ("sbuf", [128, TCOL], CODE), "bs": ("sbuf", [128, TCOL], PLANE),
     "zs": ("sbuf", [128, 4 * ZW], BF),
-    "hf": ("sbuf", [128, 4 * W1], BF), "hfq": ("sbuf", [128, W1], CODE), "hfs": ("sbuf", [128, W1], PLANE),
-    "hn": ("sbuf", [128, 4 * REST], BF), "hnq": ("sbuf", [128, max(SENT, 128)], CODE), "hns": ("sbuf", [128, max(SENT, 128)], PLANE),
     "hg": ("sbuf", [128, 512], BF), "hgq": ("sbuf", [128, 128], CODE), "hgs": ("sbuf", [128, 128], PLANE),
     "kq": ("sbuf", [128, CONST + 512], CODE), "ks": ("sbuf", [128, CONST + 512], PLANE),
-    "sn": ("sbuf", [128, 4 * WIN], F32), "sf": ("sbuf", [128, 4 * WIN], F32),
-    "yn": ("sbuf", [128, 4 * OP], F32), "yo": ("sbuf", [128, 4 * OP], F32),
+    "ho": ("sbuf", [128, 8 * UN], F32), "sn": ("sbuf", [128, 4 * WIN], F32), "wf": ("sbuf", [128, 4 * YW], F32),
+    "na": ("sbuf", [128, 4 * UN], F32), "xn": ("sbuf", [128, 4 * UN], F32), "yo": ("sbuf", [128, 4 * OP], F32),
+    "pu": ("sbuf", [128, 4], U16), "far": ("sbuf", [128, 288], BF),
 }
+for _j, _n in enumerate(SIZE):
+    SCRATCH["h%d" % _j] = ("sbuf", [128, 4 * (LEAD[_j] + max(_n, 128))], BF)
+    SCRATCH["hq%d" % _j] = ("sbuf", [128, max(_n, 128)], CODE)
+    SCRATCH["hs%d" % _j] = ("sbuf", [128, max(_n, 128)], PLANE)
 for _i in range(4):
     SCRATCH["pa%d" % _i] = ("psum", [128, 512], F32)
     SCRATCH["pb%d" % _i] = ("psum", [128, 512], F32)
 
-SEMAPHORES = (["sld", "uld", "pld", "bld", "yst", "lsend", "gi", "gtab", "gcol", "gramp", "gval",
-               "vc", "vq", "vl", "vi", "vz", "vk", "vh", "vr", "veq", "vosd", "vlst", "vbq", "vg", "vhf", "vhn", "vhg", "vinv", "vy",
-               "avals", "ah", "ar", "arrp"]
-              + [p + str(i) for p in ("ald", "vaq", "tz", "az", "tg", "tn", "tl", "am", "vn", "ayn") for i in range(4)]
-              + ["arr%d" % i for i in range(len(PLAN))])
+SEMAPHORES = (["sld", "uld", "pld", "bld", "zld", "yst", "lsend", "gi", "gtab", "gcol", "gramp", "gval",
+               "vc", "vq", "vp", "vl", "vi", "vj", "vz", "vk", "vh", "vr", "veq", "vosd", "vlst", "vbq", "vg", "vhf", "vhn", "vhg", "vinv", "vy",
+               "avals", "ah", "ar", "ao", "arrp"]
+              + [p + str(i) for p in ("ald", "vaq", "tz", "az", "tg", "tn", "tl", "am", "an", "vn", "ayn") for i in range(4)]
+              + ["arr%d" % i for i in range(len(PLAN))] + [p + str(j) for p in ("vh", "ah", "vt") for j in range(len(SIZE))])
 SHARE = {1: [[(0, 8)], [(0, 8)]], 2: [[(0, 4), (4, 4)], [(0, 4), (4, 4)]], 3: [[(0, 4), (4, 2), (6, 2)], [(4, 4), (0, 2), (2, 2)]]}
 
 
@@ -101,9 +109,9 @@ def rank_program(g, core, T, topo):
     def fill(out, pattern, base, done, step=0):
         g.iota(out, pattern, base, step, allow_small_or_imprecise_dtypes=True).then_inc(done, 1)
 
-    for k in range(2):
-        s.dma_start(T.sl[16 * k:16 * k + 16, :], T.send[:, :]).then_inc(sem.sld, 16)
-        sy.dma_start(T.ul[16 * k:16 * k + 16, :], T.un[:, :]).then_inc(sem.uld, 16)
+    for k, q in enumerate((sy, s)):
+        q.dma_start(T.sl[16 * k:16 * k + 16, :], T.send[:, :]).then_inc(sem.sld, 16)
+        q.dma_start(T.ul[16 * k:16 * k + 16, :], T.un[:, :]).then_inc(sem.uld, 16)
     sy.dma_start(T.bsb[:, :], T.b[:, :]).then_inc(sem.bld, 16)
     for i in range(4):
         sy.dma_start(T.asb[:, 512 * i:512 * i + 512], T.a[:, 512 * i:512 * i + 512]).then_inc(sem["ald%d" % i], 16)
@@ -118,6 +126,7 @@ def rank_program(g, core, T, topo):
     fill(T.ramp[:, :], [[1, 516]], -3, sem.gramp, -4)
     fill(T.val[:, :], [[0, 2], [1, UN]], 0, sem.gval)
     g.iota(T.ek[:, :], [[16, 6]], 208, 0).then_inc(sem.gval, 1)
+    fill(T.far[:, :], [[1, 288]], UN - OP, sem.gval)
 
     ch("vl", v.memset(T.row[:, :], float(TCOL)))
     ch("vz", v.memset(T.zs[:, TCOL:4 * ZW:ZW], 0.0))
@@ -125,8 +134,9 @@ def rank_program(g, core, T, topo):
     ch("vc", v.tensor_scalar(T.h16[:, :], T.ipm[:, :], 16, None, band))
     ch("vc", v.tensor_scalar(T.h8[:, :], T.ipm[:, :], 8, None, band))
     ch("vq", v.tensor_scalar(T.q15[:, :], T.ipm[:, :], 15, None, band))
-    if FIRST < W1:
-        ch("vh", v.memset(T.hf[:, 4 * FIRST:4 * W1], 0.0))
+    for j, n in enumerate(SIZE):
+        if n < 128:
+            ch("vh%d" % j, v.memset(T["h%d" % j][:, 4 * (LEAD[j] + n):4 * (LEAD[j] + 128)], 0.0))
     own("vc")
     ch("vc", v.tensor_scalar(T.sh[:, :], T.h16[:, :], -1, 16, mult, add))
     ch("vc", v.tensor_scalar(T.up[:, :], T.h8[:, :], -0.125, 1, mult, add))
@@ -137,43 +147,54 @@ def rank_program(g, core, T, topo):
     v.wait_ge(sem.gtab, 4)
     ch("vc", v.tensor_scalar(T.w1[0:32, :], T.tab[0:32, 0:24:2], T.up[0:32, 0:1], T.sh[0:32, 0:1], mult, add))
     ch("vc", v.tensor_scalar(T.w2[0:32, :], T.tab[0:32, 1:24:2], T.dn[0:32, 0:1], None, mult))
-    ch("vq", v.tensor_scalar(T.g1[:, :], T.q15[:, :], 16, T.sh[:, 0:1], mult, add))
 
-    def quantise_a(i):
-        v.wait_ge(sem["ald%d" % i], 16)
-        v.quantize_mx(T.aq[:, 128 * i:128 * i + 128], T.asc[:, 128 * i:128 * i + 128],
-                      T.asb[:, 512 * i:512 * i + 512]).then_inc(sem["vaq%d" % i], 1)
+    def step(name):
+        if name[0] == "a":
+            i = int(name[1])
+            v.wait_ge(sem["ald%d" % i], 16)
+            v.quantize_mx(T.aq[:, 128 * i:128 * i + 128], T.asc[:, 128 * i:128 * i + 128],
+                          T.asb[:, 512 * i:512 * i + 512]).then_inc(sem["vaq%d" % i], 1)
+        elif name == "b":
+            v.wait_ge(sem.bld, 16)
+            v.quantize_mx(T.bq[:, :], T.bs[:, :], T.bsb[:, :]).then_inc(sem.vbq, 1)
+        elif name[0] == "s":
+            v.wait_ge(sem.sld, 32)
+            for q in quarters[2 * int(name[1]):2 * int(name[1]) + 2]:
+                v.tensor_copy(T.osd[q, :], T.sl[0:32, :]).then_inc(sem.vosd, 1)
+        elif name == "base":
+            own("vc")
+            ch("vc", v.tensor_tensor(T.base[0:32, :], T.w1[0:32, :], T.w2[0:32, :], add))
+        elif name == "g":
+            ch("vq", v.tensor_scalar(T.g1[:, :], T.q15[:, :], 16, T.sh[:, 0:1], mult, add))
+        elif name == "pick":
+            own("vq")
+            ch("vp", v.tensor_copy(T.pick[:, 0:1], T.g1[:, 0:1]))
+            ch("vp", v.tensor_scalar(T.pick[:, 1:2], T.g1[:, 1:2], 256, 400, add, AluOpType.min))
+        elif name == "un":
+            v.wait_ge(sem.uld, 32)
+            own("vc")
+            ch("vc", v.tensor_tensor(T.x2[0:32, :], T.ul[0:32, :], T.base[0:32, :], add))
+        elif name == "pos":
+            own("vc")
+            for q in quarters:
+                ch("vl", v.tensor_copy(T.pos[q, :], T.x2[0:32, :]))
+        elif name == "row":
+            own("vl")
+            v.wait_ge(sem.avals, 1)
+            ch("vl", v.tensor_copy(T.row[:, :].indirect(T.pos[:, :]), T.vals[:, :]))
+        elif name == "turn":
+            own("vl")
+            ch("vl", v.transpose(T.rowt[:, :], T.row[:, :]))
+        elif name == "list":
+            own("vp")
+            own("vl")
+            v.tensor_copy(T.lst[:, :], T.rowt[:, :].indirect(T.pick[:, :])).then_inc(sem.vlst, 1)
 
-    v.wait_ge(sem.sld, 32)
-    for q in quarters:
-        v.tensor_copy(T.osd[q, :], T.sl[0:32, :]).then_inc(sem.vosd, 1)
+    for name in ORDER:
+        step(name)
     s.wait_ge(sem.gcol, 1)
     s.wait_ge(sem.vosd, 4)
     s.activation(T.vals[:, :], T.cols[:, :].indirect(T.osd[:, :]), copy).then_inc(sem.avals, 1)
-    own("vc")
-    ch("vc", v.tensor_tensor(T.base[0:32, :], T.w1[0:32, :], T.w2[0:32, :], add))
-    own("vq")
-    ch("vl", v.tensor_copy(T.pick[:, 0:1], T.g1[:, 0:1]))
-    ch("vl", v.tensor_scalar(T.pick[:, 1:2], T.g1[:, 1:2], 256, 400, add, AluOpType.min))
-    v.wait_ge(sem.uld, 32)
-    own("vc")
-    ch("vc", v.tensor_tensor(T.x2[0:32, :], T.ul[0:32, :], T.base[0:32, :], add))
-    v.wait_ge(sem.bld, 16)
-    v.quantize_mx(T.bq[:, :], T.bs[:, :], T.bsb[:, :]).then_inc(sem.vbq, 1)
-    own("vc")
-    for q in quarters:
-        ch("vl", v.tensor_copy(T.pos[q, :], T.x2[0:32, :]))
-    quantise_a(0)
-    own("vl")
-    v.wait_ge(sem.avals, 1)
-    ch("vl", v.tensor_copy(T.row[:, :].indirect(T.pos[:, :]), T.vals[:, :]))
-    quantise_a(1)
-    own("vl")
-    ch("vl", v.transpose(T.rowt[:, :], T.row[:, :]))
-    quantise_a(2)
-    own("vl")
-    v.tensor_copy(T.lst[:, :], T.rowt[:, :].indirect(T.pick[:, :])).then_inc(sem.vlst, 1)
-    quantise_a(3)
 
     te.wait_ge(sem.vbq, 1)
     for i in range(4):
@@ -185,117 +206,125 @@ def rank_program(g, core, T, topo):
         s.wait_ge(sem["tz%d" % i], 1)
         s.activation(T.zs[:, ZW * i:ZW * i + TCOL], T["pa%d" % i][:, 0:TCOL], copy).then_inc(sem["az%d" % i], 1)
 
-    def first(i):
-        return T.hf[:, i:4 * FIRST:4], T.zs[:, ZW * i:ZW * i + TCOL + 1].indirect(T.lst[:, 0:FIRST // 16])
+    known = {"s": set(), "v": set()}
 
-    def rest(i):
-        return T.hn[:, i:4 * REST:4], T.zs[:, ZW * i:ZW * i + TCOL + 1].indirect(T.lst[:, K2:24])
-
-    def on_scalar(pair, done):
-        s.activation(pair[0], pair[1], copy).then_inc(done, 1)
+    def into_slots(who, name):
+        q = s if who == "s" else v
+        i = int(name[1])
+        if i not in known[who]:
+            q.wait_ge(sem["az%d" % i], 1)
+            known[who].add(i)
+        window = T.zs[:, ZW * i:ZW * i + TCOL + 1]
+        if name[0] == "k":
+            s.activation(T.ho[:, 2 * UN * i:2 * UN * (i + 1)], window.indirect(T.lst[:, K3:K3 + 6]), copy).then_inc(sem.ao, 1)
+            return
+        j = int(name[0])
+        out = T["h%d" % j][:, i:4 * (LEAD[j] + SIZE[j]):4]
+        picked = window.indirect(T.lst[:, (FROM[j] - LEAD[j]) // 16:FROM[j + 1] // 16])
+        if who == "s":
+            s.activation(out, picked, copy).then_inc(sem["ah%d" % j], 1)
+        else:
+            ch("vh%d" % j, v.tensor_copy(out, picked))
 
     for i in range(4):
         leave(i)
     s.wait_ge(sem.vlst, 1)
     s.wait_ge(sem.vz, 1)
-    s.wait_ge(sem.az0, 1)
-    s.wait_ge(sem.az1, 1)
-    on_scalar(rest(0), sem.ar)
-    on_scalar(rest(1), sem.ar)
-
+    for name in ON_SCALAR + ["k%d" % i for i in range(4)]:
+        into_slots("s", name)
     v.wait_ge(sem.vlst, 1)
     own("vz")
-    for i in range(4):
-        v.wait_ge(sem["az%d" % i], 1)
-        ch("vh", v.tensor_copy(*first(i)))
-    own("vh")
-    v.quantize_mx(T.hfq[:, :], T.hfs[:, :], T.hf[:, :]).then_inc(sem.vhf, 1)
-    ch("vr", v.tensor_copy(*rest(2)))
-    ch("vr", v.tensor_copy(*rest(3)))
-    v.wait_ge(sem.gramp, 1)
-    ch("vk", v.tensor_scalar(T.cst[:, :], T.ramp[:, :], 0, None, AluOpType.is_equal))
-    v.wait_ge(sem.ar, 2)
-    own("vr")
-    if SENT:
-        v.quantize_mx(T.hnq[:, :], T.hns[:, :], T.hn[:, 4 * LEAD:4 * (LEAD + SENT)]).then_inc(sem.vhn, 1)
+    for name in ON_VECTOR:
+        if name == "cst":
+            v.wait_ge(sem.gramp, 1)
+            ch("vk", v.tensor_scalar(T.cst[:, :], T.ramp[:, :], 0, None, AluOpType.is_equal))
+        elif name == "zero":
+            ch("vg", v.memset(T.hg[:, :], 0.0))
+        elif name[0] == "q":
+            j, n = int(name[1]), sum(x[0] == name[1] for x in ON_SCALAR)
+            if n:
+                v.wait_ge(sem["ah%d" % j], n)
+            own("vh%d" % j)
+            v.quantize_mx(T["hq%d" % j][:, :], T["hs%d" % j][:, :],
+                          T["h%d" % j][:, 4 * LEAD[j]:4 * (LEAD[j] + max(SIZE[j], 128))]).then_inc(sem["vt%d" % j], 1)
+        else:
+            into_slots("v", name)
 
     sent = 16
     for i, step in enumerate(PLAN):
-        if i < 2:
-            g.wait_ge(sem.vhn if i else sem.vhf, 1)
+        if TILE.index(TILE[i]) == i:
+            g.wait_ge(sem["vt%d" % TILE[i]], 1)
         for k in range(2):
             call = []
             for j, (n, kinds) in enumerate(step):
                 blk, width, d = (kinds[0], n), UN * len(kinds), peer[n]
                 rid, pid = topo.addr(d, core)
                 e0, count = SHARE[len(step)][k][j]
-                src = side(T, "hnq", "hns", k, SLOT[blk] - FIRST, width) if i else side(T, "hfq", "hfs", k, SLOT[blk], width)
-                call.append(RemoteDMATransfer(
-                    dst_ids=[DstId(rid=rid, pnc=pid)], dma_engine_mask=sum(1 << e for e in topo.engines(core, d)[e0:e0 + count]),
-                    remote_sem=sem["arr%d" % i], src=src, dst=side(T, "kq", "ks", k, AT[blk], width)))
-            g.remote_dma_fused(call, local_sem=sem.lsend)
-            sent += 8
+                engines = topo.engines(core, d)[k::2] if i < SPLIT else topo.engines(core, d)[e0:e0 + count]
+                src = side(T, "hq%d" % TILE[i], "hs%d" % TILE[i], k, SLOT[blk] - FROM[TILE[i]], width)
+                dst, mask = side(T, "kq", "ks", k, AT[blk], width), sum(1 << e for e in engines)
+                sent += len(engines)
+                if len(step) == 1:
+                    g.remote_dma(dst, src, sem["arr%d" % i], sem.lsend, pid, rid, mask)
+                else:
+                    call.append(RemoteDMATransfer(dst_ids=[DstId(rid=rid, pnc=pid)], dma_engine_mask=mask,
+                                                  remote_sem=sem["arr%d" % i], src=src, dst=dst))
+            if call:
+                g.remote_dma_fused(call, local_sem=sem.lsend)
 
     def constant(t):
         a = CONST + 128 * t
         v.quantize_mx(T.kq[:, a:a + 128], T.ks[:, a:a + 128], T.cst[:, 3 - t:515 - t]).then_inc(sem.veq, 1)
 
     own("vk")
+    for t in range(4):
+        constant(t)
+    own("vg")
+    v.quantize_mx(T.kq[:, CONST - 128:CONST], T.ks[:, CONST - 128:CONST], T.hg[:, :]).then_inc(sem.veq, 1)
     v.wait_ge(sem.pld, 32)
-    v.wait_ge(sem.gval, 2)
+    v.wait_ge(sem.gval, 3)
     own("vi")
+    gf = topo.host(partner)
     for q in quarters:
         ch("vi", v.tensor_scalar(T.p1[q, :], T.pl[0:32, :], 511, None, band))
     ch("vi", v.tensor_scalar(T.dump[:, :], T.ek[:, :], T.qf[:, 0:1], None, add))
-    ch("vi", v.memset(T.inv[:, :], float(UN)))
-    constant(0)
+    ch("vj", v.tensor_scalar(T.inv[:, 0:288], T.far[:, :], T.sh[:, 0:1], UN, AluOpType.subtract, AluOpType.max))
     own("vi")
     ch("vi", v.tensor_tensor(T.p2[:, :], T.p1[:, :], T.dump[:, :], AluOpType.min))
-    constant(1)
+    ch("vz", v.memset(T.sn[:, UN:4 * WIN:WIN], 0.0))
+    ch("vz", v.tensor_copy(T.pu[quarters[3], 0:3], T.pl[0:32, 3 * gf:3 * gf + 3]))
     own("vi")
     for h in range(2):
-        ch("vi", v.tensor_scalar(T.po[:, 3 * h:3 * h + 3], T.p2[:, 3 * h:3 * h + 3], T.sh[:, 0:1], OP * h, add, add))
-    constant(2)
-    constant(3)
-    own("vi")
+        ch("vj", v.tensor_scalar(T.po[:, 3 * h:3 * h + 3], T.p2[:, 3 * h:3 * h + 3], T.sh[:, 0:1], OP * (h == gf), add, add))
+    for q in quarters[:3]:
+        ch("vz", v.tensor_copy(T.pu[q, 0:3], T.pl[0:32, 3 * gf:3 * gf + 3]))
+    own("vj")
     ch("vi", v.tensor_copy(T.inv[:, :].indirect(T.po[:, :]), T.val[:, :]))
-    ch("vg", v.memset(T.hg[:, 0:320], 0.0))
-    own("vi")
-    ch("vi", v.transpose(T.invt[:, :], T.inv[:, 0:288]))
-    ch("vz", v.memset(T.sn[:, UN:4 * WIN:WIN], 0.0))
-    ch("vz", v.memset(T.sf[:, UN:4 * WIN:WIN], 0.0))
-    own("vi")
-    own("vz")
-    v.tensor_copy(T.offi[:, :], T.invt[:, :].indirect(T.pick[:, 0:1])).then_inc(sem.vinv, 1)
 
-    def unpack(bank, t, blk, start, stop):
-        a, c = CONST + 128 * t, AT[blk]
-        return te.matmul_mx(T[bank + str(t)][:, 0:128], T.kq[:, a:a + 128], T.ks[:, a:a + 128],
-                            T.kq[:, c:c + 128], T.ks[:, c:c + 128], start, stop)
-
-    def add_up(kind, bank, done):
-        seen = 0
-        for i, step in enumerate(STEPS):
-            landed = [blk for blk in step if blk[0] == kind]
-            te.wait_ge(sem["arr%d" % i], 16)
-            for t in range(4):
-                for j, blk in enumerate(landed):
-                    ins = unpack(bank, t, blk, seen + j == 0, seen + j == 2)
-                    if seen + j == 2:
-                        ins.then_inc(sem[done + str(t)], 1)
-            seen += len(landed)
-            if seen == 3:
-                return
+    def unpack(bank, step, start, stop, done=None):
+        c = AT[step[0]]
+        for t in range(4):
+            a = CONST + 128 * t
+            ins = te.matmul_mx(T[bank + str(t)][:, 0:128], T.kq[:, a:a + 128], T.ks[:, a:a + 128],
+                               T.kq[:, c:c + 128], T.ks[:, c:c + 128], start, stop)
+            if done:
+                ins.then_inc(sem[done + str(t)], 1)
 
     def mine(kind, t):
-        a = 4 * (SLOT[kind, OWN] - 16 * K2)
-        return T.hn[:, a + t:a + 4 * UN:4]
+        a = 2 * UN * t + SLOT[kind, OWN] - 16 * K3
+        return T.ho[:, a:a + UN]
 
-    te.wait_ge(sem.veq, 4)
-    add_up("f", "pb", "tg")
+    te.wait_ge(sem.veq, 5)
+    for i in range(3):
+        te.wait_ge(sem["arr%d" % i], 8 if i < SPLIT else 16)
+        unpack("pb", STEPS[i], i == 0, i == 2, "tg" if i == 2 else None)
+
+    v.wait_ge(sem.ao, 4)
     for t in range(4):
         v.wait_ge(sem["tg%d" % t], 1)
         ch("vg", v.tensor_tensor(T.hg[:, 320 + t:512:4], T["pb%d" % t][:, 0:UN], mine("f", t), add))
+    own("vi")
+    ch("vi", v.transpose(T.invt[:, :], T.inv[:, 0:288]))
     own("vg")
     v.quantize_mx(T.hgq[:, :], T.hgs[:, :], T.hg[:, :]).then_inc(sem.vhg, 1)
     rid, pid = topo.addr(partner, core)
@@ -304,30 +333,42 @@ def rank_program(g, core, T, topo):
         g.remote_dma(side(T, "kq", "ks", k, AT["p", 0]), side(T, "hgq", "hgs", k, 128 - UN), sem.arrp, sem.lsend,
                      pid, rid, topo.mask(core, partner))
 
+    for t in range(4):
+        ch("vg", v.tensor_tensor(T.xn[:, UN * t:UN * t + UN], T["pb%d" % t][:, UN:2 * UN], mine("n", t), add))
+    own("vi")
+    ch("vz", v.tensor_copy(T.offi[:, :], T.invt[:, :].indirect(T.pick[:, 0:1])))
     for i in range(4):
         te.wait_ge(sem["az%d" % i], 1)
-    add_up("n", "pa", "tn")
-    gn, gf = 6 * topo.host(core), 6 * topo.host(partner)
-    s.wait_ge(sem.vinv, 1)
+    te.wait_ge(sem.arr3, 16)
+    unpack("pa", STEPS[3], True, True, "tn")
+    own("vg")
+    def gather(t, need, out, window, done):
+        q = s if t < 2 else v
+        q.wait_ge(sem[need + str(t)], 1)
+        (s.activation(out, window, copy) if t < 2 else v.tensor_copy(out, window)).then_inc(done, 1)
+
     for t in range(4):
         v.wait_ge(sem["tn%d" % t], 1)
-        v.tensor_tensor(T.sn[:, WIN * t:WIN * t + UN], T["pa%d" % t][:, 0:UN], mine("n", t), add).then_inc(sem["vn%d" % t], 1)
-        s.wait_ge(sem["vn%d" % t], 1)
-        s.activation(T.yn[:, OP * t:OP * t + OP], T.sn[:, WIN * t:WIN * t + UN + 1].indirect(T.offi[:, gn:gn + 6]),
-                     copy).then_inc(sem["ayn%d" % t], 1)
+        v.tensor_tensor(T.sn[:, WIN * t:WIN * t + UN], T["pa%d" % t][:, 0:UN], T.xn[:, UN * t:UN * t + UN],
+                        add).then_inc(sem["vn%d" % t], 1)
+    s.wait_ge(sem.vz, cnt["vz"])
+    own("vz")
+    for t in range(4):
+        gather(t, "vn", T.wf[:, YW * t + UN:YW * (t + 1)], T.sn[:, WIN * t:WIN * t + UN + 1].indirect(T.offi[:, 0:6]),
+               sem["ayn%d" % t])
+    for t in range(4):
+        gather(t, "ayn", T.na[:, UN * t:UN * t + UN], T.wf[:, YW * t + UN:YW * (t + 1)].indirect(T.pu[:, 0:3]), sem["an%d" % t])
 
     te.wait_ge(sem.arrp, 16)
     te.wait_ge(sem.vg, cnt["vg"])
+    unpack("pb", [("p", 0)], True, True, "tl")
     for t in range(4):
-        unpack("pb", t, ("p", 0), True, True).then_inc(sem["tl%d" % t], 1)
-        s.wait_ge(sem["tl%d" % t], 1)
-        s.activation(T.sf[:, WIN * t:WIN * t + UN], T["pb%d" % t][:, 0:UN], copy).then_inc(sem["am%d" % t], 1)
-    v.wait_ge(sem.vinv, 1)
+        v.wait_ge(sem["an%d" % t], 1)
+        v.wait_ge(sem["tl%d" % t], 1)
+        v.tensor_tensor(T.wf[:, YW * t:YW * t + UN], T["pb%d" % t][:, 0:UN], T.na[:, UN * t:UN * t + UN],
+                        add).then_inc(sem["am%d" % t], 1)
     for t in range(4):
-        v.wait_ge(sem["ayn%d" % t], 1)
-        v.wait_ge(sem["am%d" % t], 1)
-        v.tensor_tensor(T.yo[:, t:4 * OP:4], T.sf[:, WIN * t:WIN * t + UN + 1].indirect(T.offi[:, gf:gf + 6]),
-                        T.yn[:, OP * t:OP * t + OP], add).then_inc(sem.vy, 1)
+        gather(t, "am", T.yo[:, t:4 * OP:4], T.wf[:, YW * t:YW * (t + 1)].indirect(T.offi[:, 6:12]), sem.vy)
     sy.wait_ge(sem.vy, 4)
     sy.dma_start(T.y[:, :], T.yo[:, 0:4 * OC]).then_inc(sem.yst, 16)
     sy.wait_ge(sem.yst, 16)

@@ -1,74 +1,82 @@
-from concourse.bass import DstId, RemoteDMATransfer
 from concourse.mybir import dt, AluOpType, ActivationFunctionType
 
 N, TCOL, CAPP, OC, UN = 8, 192, 24, 88, 48
 H = 4
-ZW = 208
-ROW = 416
-OP = 96
-WIN = 56
-
-PLAN = [[(0, "f")], [(1, "fn")], [(2, "fn")], [(0, "n")]]
 OWN = H - 1
-BLOCKS = [(kind, n) for step in PLAN for n, kinds in step for kind in kinds] + [("n", OWN), ("f", OWN)]
-SLOT = {blk: UN * i for i, blk in enumerate(BLOCKS)}
-SPLIT = 1
-TILE = [0, 1, 2, 2]
-FROM = [SLOT[PLAN[TILE.index(j)][0][1][0], PLAN[TILE.index(j)][0][0]] for j in range(max(TILE) + 1)] + [SLOT["n", OWN]]
-SIZE = [b - a for a, b in zip(FROM, FROM[1:])]
-LEAD = [a % 32 for a in FROM]
-K3 = SLOT["n", OWN] // 16
-YW = UN + OP
-ON_VECTOR = "00 01 03 q0 12 13 cst q1 23 zero q2".split()
-ON_SCALAR = "02 10 11 20 21 22".split()
-STEPS = [[(kind, n) for n, kinds in step for kind in kinds] for step in PLAN]
-LANDS = [("p", 0)] + [blk for step in STEPS[::-1] for blk in step]
-AT = {blk: UN * i for i, blk in enumerate(LANDS)}
-CONST = UN * len(LANDS) + 128
+ZW = 208
+SLOT = [0, 64, 112, 176]
+ROW = 256
+OP = 96
+YW = 104
+IW = 144
+LOW, HIGH = 7, 120
+BW = TCOL + 6
 
-ORDER = "g s0 base s1 un pick pos b a0 row a1 a2 turn a3 list".split()
+TILES = [("f", 0, 1), ("f", 1, 2), ("n", 0, 1), ("n", 1, 2), ("f", 3, 1), ("s", 0, 1), ("n", 3, 1)]
+WRITES = ["f0", "f1", "f2", "n0", "n1", "n2"]
+RELAY = []
+LANDS = ["f0", "f1", "f2", "n0", "n1", "n2"]
+
+ORDER = "un pick pos low high blank parts b a0 rowf a1 a2 turnf a3 listf 00 z3 03 q0 rown 13 turnn q1 listn 22 23 q2 32 33 q3 42 43".split()
+ON_SCALAR = "valf valn z0 z1 z2 02 01 10 11 12 20 21 30 31 40 41 60 61 62 63".split()
+LAST = [(0, 6, 12), (12, 16, 22)]
+
+
+def layout():
+    span = [(SLOT[a] // 32 * 32, SLOT[a + n - 1] + UN) for kind, a, n in TILES]
+    start = max(TCOL // 4, 128 - span[0][1] + span[0][0])
+    end, at = [], start
+    for a, b in span:
+        at += b - a
+        end.append(at)
+    where = {kind + str(i): (j, end[j] - span[j][1] + SLOT[i]) for j, (kind, a, n) in enumerate(TILES) for i in range(a, a + n)}
+    return span, start, end, where
+
+
+SPAN, START, END, WHERE = layout()
+SUM = WHERE["s0"][0]
+QW = 192
+AT = {blk: UN * (len(LANDS) - i) for i, blk in enumerate(LANDS)}
+CONST = UN * (len(LANDS) + 1)
+LISTS = CONST + 512
+TURN = LISTS + 28
 
 F32, BF, I32, U16 = "float32", "bfloat16", "int32", "uint16"
 CODE, PLANE = "float8_e4m3fn_x4", "uint8"
 SCRATCH = {
-    "asb": ("sbuf", [128, 2048], BF), "bsb": ("sbuf", [128, 4 * TCOL], BF),
-    "sl": ("sbuf", [128, 12], I32), "ul": ("sbuf", [128, 12], I32), "pl": ("sbuf", [128, 6], I32),
-    "ramp": ("sbuf", [128, 516], BF), "cst": ("sbuf", [128, 516], BF),
-    "ipm": ("sbuf", [128, 2], I32), "ek": ("sbuf", [128, 6], I32), "q15": ("sbuf", [128, 2], I32),
-    "h16": ("sbuf", [128, 2], I32), "h8": ("sbuf", [128, 2], I32), "qf": ("sbuf", [128, 2], F32),
-    "sh": ("sbuf", [128, 2], F32), "up": ("sbuf", [128, 2], F32), "dn": ("sbuf", [128, 2], F32),
-    "tab": ("sbuf", [128, 24], I32), "w1": ("sbuf", [128, 12], I32),
-    "w2": ("sbuf", [128, 12], I32),
-    "base": ("sbuf", [128, 12], I32), "x2": ("sbuf", [128, 12], I32), "g1": ("sbuf", [128, 2], I32),
-    "dump": ("sbuf", [128, 6], I32), "p1": ("sbuf", [128, 6], I32), "p2": ("sbuf", [128, 6], I32),
-    "osd": ("sbuf", [128, 12], U16), "pos": ("sbuf", [128, 12], U16), "po": ("sbuf", [128, 6], U16),
-    "pick": ("sbuf", [128, 2], U16), "lst": ("sbuf", [128, 32], U16), "offi": ("sbuf", [128, 16], U16),
-    "cols": ("sbuf", [128, TCOL], BF), "vals": ("sbuf", [128, TCOL], BF), "val": ("sbuf", [128, 2 * UN], BF),
-    "row": ("sbuf", [128, ROW], BF), "rowt": ("sbuf", [128, ROW], BF),
-    "inv": ("sbuf", [128, ROW], BF), "invt": ("sbuf", [128, 288], BF),
+    "asb": ("sbuf", [128, 2048], BF), "bsb": ("sbuf", [128, 4 * BW], BF),
+    "su": ("sbuf", [128, 24], I32), "pl": ("sbuf", [128, 6], I32), "pp": ("sbuf", [128, 12], I32),
+    "ipm": ("sbuf", [128, 2], I32), "p16": ("sbuf", [128, 2], I32), "bits": ("sbuf", [128, 8], I32), "col": ("sbuf", [128, 8], F32),
+    "tab": ("sbuf", [128, 12], I32), "base": ("sbuf", [128, 12], I32),
+    "off": ("sbuf", [128, 24], U16), "pick": ("sbuf", [128, 2], U16), "lst": ("sbuf", [128, 32], U16),
+    "offi": ("sbuf", [128, 28], U16), "vals": ("sbuf", [128, TCOL], BF),
+    "row": ("sbuf", [128, 2 * ROW], BF), "rowt": ("sbuf", [128, 2 * ROW], BF),
     "aq": ("sbuf", [128, 512], CODE), "asc": ("sbuf", [128, 512], PLANE),
-    "bq": ("sbuf", [128, TCOL], CODE), "bs": ("sbuf", [128, TCOL], PLANE),
-    "zs": ("sbuf", [128, 4 * ZW], BF),
-    "hg": ("sbuf", [128, 512], BF), "hgq": ("sbuf", [128, 128], CODE), "hgs": ("sbuf", [128, 128], PLANE),
-    "kq": ("sbuf", [128, CONST + 512], CODE), "ks": ("sbuf", [128, CONST + 512], PLANE),
-    "ho": ("sbuf", [128, 8 * UN], F32), "sn": ("sbuf", [128, 4 * WIN], F32), "wf": ("sbuf", [128, 4 * YW], F32),
-    "na": ("sbuf", [128, 4 * UN], F32), "xn": ("sbuf", [128, 4 * UN], F32), "yo": ("sbuf", [128, 4 * OP], F32),
-    "pu": ("sbuf", [128, 4], U16), "far": ("sbuf", [128, 288], BF),
+    "bq": ("sbuf", [128, BW], CODE), "bs": ("sbuf", [128, BW], PLANE),
+    "zs": ("sbuf", [128, 4 * ZW], BF), "hh": ("sbuf", [128, 4 * END[-1]], BF),
+    "hq": ("sbuf", [128, QW * len(TILES)], CODE), "hs": ("sbuf", [128, QW * len(TILES)], PLANE),
+    "kq": ("sbuf", [128, TURN + 128], CODE), "ks": ("sbuf", [128, TURN + 128], PLANE),
+    "wf": ("sbuf", [128, 4 * YW], F32), "na": ("sbuf", [128, 4 * UN], F32), "yo": ("sbuf", [128, 4 * OP], F32),
+    "ones": ("sbuf", [128, 516], BF), "ramp": ("sbuf", [128, 516], BF), "cst": ("sbuf", [128, 516], BF),
+    "first": ("sbuf", [128, 2], F32), "cq": ("sbuf", [128, 256], CODE), "cs": ("sbuf", [128, 256], PLANE),
+    "rq": ("sbuf", [128, UN], CODE), "rs": ("sbuf", [128, UN], PLANE),
+    "lq": ("sbuf", [128, 144], CODE), "ls": ("sbuf", [128, 144], PLANE),
+    "w16": ("sbuf", [128, 128], BF), "w4": ("sbuf", [128, 32], BF), "wl": ("sbuf", [128, 512], BF), "wr": ("sbuf", [128, 512], BF),
+    "dump": ("sbuf", [128, 6], F32), "ek": ("sbuf", [128, 6], F32), "place2": ("sbuf", [128, 6], F32),
+    "po": ("sbuf", [128, 10], U16), "cg": ("sbuf", [128, 8], U16), "e16": ("sbuf", [128, 6], F32), "val": ("sbuf", [128, 2 * UN], BF),
+    "inv": ("sbuf", [128, 2 * IW], BF), "lrow": ("sbuf", [128, 192], BF),
+    "li": ("sbuf", [128, 112], I32), "lj": ("sbuf", [128, 112], I32), "lt": ("sbuf", [128, 512], BF),
 }
-for _j, _n in enumerate(SIZE):
-    SCRATCH["h%d" % _j] = ("sbuf", [128, 4 * (LEAD[_j] + max(_n, 128))], BF)
-    SCRATCH["hq%d" % _j] = ("sbuf", [128, max(_n, 128)], CODE)
-    SCRATCH["hs%d" % _j] = ("sbuf", [128, max(_n, 128)], PLANE)
 for _i in range(4):
     SCRATCH["pa%d" % _i] = ("psum", [128, 512], F32)
     SCRATCH["pb%d" % _i] = ("psum", [128, 512], F32)
 
-SEMAPHORES = (["sld", "uld", "pld", "bld", "zld", "yst", "lsend", "gi", "gtab", "gcol", "gramp", "gval",
-               "vc", "vq", "vp", "vl", "vi", "vj", "vz", "vk", "vh", "vr", "veq", "vosd", "vlst", "vbq", "vg", "vhf", "vhn", "vhg", "vinv", "vy",
-               "avals", "ah", "ar", "ao", "arrp"]
-              + [p + str(i) for p in ("ald", "vaq", "tz", "az", "tg", "tn", "tl", "am", "an", "vn", "ayn") for i in range(4)]
-              + ["arr%d" % i for i in range(len(PLAN))] + [p + str(j) for p in ("vh", "ah", "vt") for j in range(len(SIZE))])
-SHARE = {1: [[(0, 8)], [(0, 8)]], 2: [[(0, 4), (4, 4)], [(0, 4), (4, 4)]], 3: [[(0, 4), (4, 2), (6, 2)], [(4, 4), (0, 2), (2, 2)]]}
+SEMAPHORES = (["sld", "uld", "pld", "bld", "yst", "lsend", "gi", "gtab", "gcol", "gval", "gpick", "azero", "apart",
+               "vc", "vq", "vp", "vl", "vi", "vj", "vk", "vu", "vw", "voff", "vbq", "vg", "vhg", "vy",
+               "arrp", "arrc", "arrw", "arrl", "arru", "arrr", "tu", "vinv"]
+              + [p + k for p in ("avals", "vrow", "vlst") for k in "fn"] + ["arr" + blk for blk in LANDS]
+              + [p + str(i) for p in ("ald", "vaq", "tz", "az", "tg", "tn", "tl", "am", "an", "vn", "ay") for i in range(4)]
+              + [p + str(i) for p in ("ah", "vt") for i in range(len(TILES))])
 
 
 def turn(topo, dst, src):
@@ -79,24 +87,32 @@ def turn(topo, dst, src):
     return 1 if topo.same_plane(dst, src) else 0
 
 
-def side(T, q, p, k, a, n=UN):
+def peers(T, topo, core):
+    return {turn(topo, c, core): c for c in T.cores if topo.host(c) == topo.host(core)}
+
+
+def neighbours(T, topo, home):
+    idle = [c for c in topo.cores_of(home) if c != home and topo.die(c) == topo.die(home)]
+    jobs = []
+    for blk in RELAY:
+        jobs.append([c for c in idle if c not in jobs and topo.may_write(c, peers(T, topo, home)[int(blk[1])])][0])
+    return jobs + [c for c in idle if c not in jobs]
+
+
+def side(T, q, p, k, a, n):
     return T[p][:, a:a + n] if k else T[q][:, a:a + n].bitcast(dt.uint8)
 
 
-def rank_program(g, core, T, topo):
-    rank = T.rank_of(core)
-    if rank is None:
-        return
-    v, s, te, sy, sem = g.vector, g.scalar, g.tensor, g.sync, T.sem
-    add, mult, band = AluOpType.add, AluOpType.mult, AluOpType.bitwise_and
-    copy = ActivationFunctionType.Copy
-    here = [r for r in range(N) if topo.host(T.cores[r]) == topo.host(core)]
-    there = [r for r in range(N) if topo.host(T.cores[r]) != topo.host(core)]
-    peer = {turn(topo, T.cores[r], core): T.cores[r] for r in here}
-    partner = T.cores[there[here.index(rank)]]
-    block = {r: ("n", turn(topo, T.cores[r], core)) for r in here}
-    block.update({r: ("f", block[q][1]) for r, q in zip(there, here)})
+def send(g, T, topo, core, dst, to, frm, n, arrival, engines=None):
+    rid, pid = topo.addr(dst, core)
+    engines = engines or [topo.engines(core, dst)] * 2
+    for k in range(2):
+        g.remote_dma(side(T, to[0], to[1], k, to[2], n), side(T, frm[0], frm[1], k, frm[2], n), arrival, T.sem.lsend,
+                     pid, rid, sum(1 << e for e in engines[k]))
+    return len(engines[0]) + len(engines[1])
 
+
+def chains(v, sem):
     cnt = {}
 
     def ch(name, ins):
@@ -106,203 +122,295 @@ def rank_program(g, core, T, topo):
     def own(name):
         v.wait_ge(sem[name], cnt[name])
 
-    def fill(out, pattern, base, done, step=0):
-        g.iota(out, pattern, base, step, allow_small_or_imprecise_dtypes=True).then_inc(done, 1)
+    return ch, own, cnt
+
+
+def fill(g, out, pattern, base, done, step=0):
+    g.iota(out, pattern, base, step, allow_small_or_imprecise_dtypes=True).then_inc(done, 1)
+
+
+def constants_program(g, core, T, topo, home, half):
+    v, sem = g.vector, T.sem
+    ch, own, cnt = chains(v, sem)
+    fill(g, T.first[:, :], [[0, 2]], -4, sem.gi, -4)
+    ch("vc", v.memset(T.ones[:, :], 1.0))
+    own("vc")
+    v.wait_ge(sem.gi, 1)
+    ch("vc", v.tensor_tensor_scan(T.ramp[:, :], T.ones[:, :], T.ones[:, :], T.first[:, 0:1], AluOpType.add, AluOpType.mult))
+    own("vc")
+    ch("vc", v.tensor_scalar(T.cst[:, :], T.ramp[:, :], 0, None, AluOpType.is_equal))
+    own("vc")
+    for k in range(2):
+        t, a = 2 * half + k, 128 * k
+        ch("vk", v.quantize_mx(T.cq[:, a:a + 128], T.cs[:, a:a + 128], T.cst[:, 3 - t:515 - t]))
+    g.wait_ge(sem.vk, cnt["vk"])
+    sent = send(g, T, topo, core, home, ("kq", "ks", CONST + 256 * half), ("cq", "cs", 0), 256, sem.arrc)
+    if half < len(RELAY):
+        blk = RELAY[half]
+        g.wait_ge(sem.arrr, 16)
+        sent += send(g, T, topo, core, peers(T, topo, home)[int(blk[1])], ("kq", "ks", AT[blk]), ("rq", "rs", 0), UN, sem["arr" + blk])
+    g.wait_ge(sem.lsend, sent)
+
+
+def lists_program(g, core, T, topo, home, far):
+    v, te, sem = g.vector, g.tensor, T.sem
+    add, mult, band, low = AluOpType.add, AluOpType.mult, AluOpType.bitwise_and, AluOpType.min
+    ch, own, cnt = chains(v, sem)
+    g.iota(T.ipm[:, :], [[0, 2]], 0, 1).then_inc(sem.gi, 1)
+    fill(g, T.w4[:, :], [[0, 8], [16, 4]], 0, sem.gtab, -1)
+    fill(g, T.w16[:, :], [[0, 8], [1, 16]], 0, sem.gcol, -1)
+    fill(g, T.ek[:, :], [[0, 2], [16, 3]], OC, sem.gval)
+    fill(g, T.e16[:, :], [[16, 6]], 0, sem.gval)
+    fill(g, T.val[:, :], [[UN * (1 - 2 * far), 2], [1, UN]], UN * far, sem.gval)
+    ch("vw", v.memset(T.wr[:, :], 0.0))
+    ch("vl", v.memset(T.wl[:, :], 0.0))
+    v.wait_ge(sem.gi, 1)
+    for k, m in enumerate((15, 12, 3, 48, 64)):
+        ch("vc", v.tensor_scalar(T.bits[:, k:k + 1], T.ipm[:, 0:1], m, None, band))
+    own("vc")
+    ch("vw", v.tensor_scalar(T.col[:, 6:7], T.bits[:, 4:5], -1, None, mult))
+    own("vw")
+    v.wait_ge(sem.gtab, 1)
+    for t in range(4):
+        ch("vw", v.tensor_scalar(T.wr[:, 5 * t:512:16], T.w4[:, :], T.col[:, 6:7], None, AluOpType.is_equal))
+    own("vw")
+    v.quantize_mx(T.cq[:, 0:128], T.cs[:, 0:128], T.wr[:, :]).then_inc(sem.vk, 1)
+    g.wait_ge(sem.vk, 1)
+    sent = send(g, T, topo, core, home, ("kq", "ks", TURN), ("cq", "cs", 0), 128, sem.arrw)
+    own("vl")
+    v.wait_ge(sem.gcol, 1)
+    for t in range(2):
+        ch("vl", v.tensor_scalar(T.wl[:, t:512:4], T.w16[:, :], 0, None, AluOpType.is_equal))
+    own("vc")
+    ch("vc", v.tensor_copy(T.col[:, 0:4], T.bits[:, 0:4]))
+    ch("vi", v.memset(T.inv[:, :], float(2 * UN)))
+    ch("vj", v.memset(T.lrow[:, :], 0.0))
+    ch("vu", v.memset(T.lt[:, :], 0.0))
+    own("vl")
+    v.quantize_mx(T.lq[:, 16:144], T.ls[:, 16:144], T.wl[:, :]).then_inc(sem.vq, 1)
+    own("vc")
+    v.wait_ge(sem.gval, 3)
+    ch("vc", v.tensor_scalar(T.dump[:, :], T.ek[:, :], T.col[:, 0:1], None, add))
+    ch("vc", v.tensor_scalar(T.col[:, 4:5], T.col[:, 1:2], 4, T.col[:, 2:3], mult, add))
+    ch("vc", v.tensor_scalar(T.col[:, 7:8], T.col[:, 3:4], 1 / 16, T.col[:, 1:2], mult, add))
+    own("vc")
+    ch("vc", v.tensor_scalar(T.col[:, 5:6], T.col[:, 3:4], 0.25, T.col[:, 4:5], mult, add))
+    own("vc")
+    ch("vp", v.tensor_scalar(T.cg[:, 0:6], T.e16[:, :], T.col[:, 7:8], None, add))
+    ch("vp", v.tensor_scalar(T.cg[:, 6:7], T.col[:, 5:6], OP, None, add))
+
+    te.wait_ge(sem.vq, 1)
+    te.wait_ge(sem.arru, 16)
+    te.matmul_mx(T.pa0[:, 0:128], T.lq[:, 16:144], T.ls[:, 16:144], T.lq[:, 10:138], T.ls[:, 10:138], True, True).then_inc(sem.tu, 1)
+    v.wait_ge(sem.tu, 1)
+    ch("vc", v.tensor_tensor(T.place2[:, :], T.pa0[:, 0:6], T.dump[:, :], low))
+    own("vc")
+    for h in range(2):
+        ch("vi", v.tensor_scalar(T.po[:, 3 * h:3 * h + 3], T.place2[:, 3 * h:3 * h + 3], IW * (h == far), None, add))
+    ch("vi", v.tensor_copy(T.po[:, 6:9], T.place2[:, 3 * far:3 * far + 3]))
+    own("vi")
+    ch("vi", v.tensor_copy(T.inv[:, :].indirect(T.po[:, 0:6]), T.val[:, :]))
+    own("vi")
+    own("vj")
+    ch("vj", v.tensor_tensor(T.lrow[:, 0:OP], T.inv[:, 0:OP], T.inv[:, IW:IW + OP], low))
+    ch("vj", v.tensor_scalar(T.lrow[:, OP:OP + UN], T.inv[:, 0:IW].indirect(T.po[:, 6:9]), -UN, None, add))
+    own("vj")
+    own("vp")
+    ch("vj", v.tensor_copy(T.li[:, :], T.lrow[:, :].indirect(T.cg[:, 0:7])))
+    own("vj")
+    for h, m in enumerate((LOW, HIGH)):
+        ch("vj", v.tensor_scalar(T.lj[64 * h:64 * h + 64, :], T.li[64 * h:64 * h + 64, :], m, None, band))
+    own("vj")
+    own("vu")
+    ch("vu", v.tensor_copy(T.lt[:, 0:112], T.lj[:, :]))
+    own("vu")
+    v.quantize_mx(T.cq[:, 128:256], T.cs[:, 128:256], T.lt[:, :]).then_inc(sem.vk, 1)
+    g.wait_ge(sem.vk, 2)
+    sent += send(g, T, topo, core, home, ("kq", "ks", LISTS), ("cq", "cs", 128), TURN - LISTS, sem.arrl)
+    g.wait_ge(sem.lsend, sent)
+
+
+def rank_program(g, core, T, topo):
+    rank = T.rank_of(core)
+    if rank is None:
+        for home in T.cores:
+            if core in neighbours(T, topo, home):
+                job = neighbours(T, topo, home).index(core)
+                if job < 2:
+                    constants_program(g, core, T, topo, home, job)
+                else:
+                    lists_program(g, core, T, topo, home, 1 - topo.host(home))
+        return
+    v, s, te, sy, sem = g.vector, g.scalar, g.tensor, g.sync, T.sem
+    add, mult, band = AluOpType.add, AluOpType.mult, AluOpType.bitwise_and
+    copy = ActivationFunctionType.Copy
+    here = [r for r in range(N) if topo.host(T.cores[r]) == topo.host(core)]
+    there = [r for r in range(N) if topo.host(T.cores[r]) != topo.host(core)]
+    peer, helper = peers(T, topo, core), neighbours(T, topo, core)
+    partner = T.cores[there[here.index(rank)]]
+    link = topo.engines(core, partner)
+    rest = [e for e in topo.engines(core, helper[0]) if e not in link]
+    first = [SLOT[turn(topo, T.cores[r], core)] for r in here]
+    d1, d2 = first[1] - first[0], first[2] - first[0]
+    assert first[3] == first[0] + d1 + d2
+    half = {"f": there[0] // H, "n": here[0] // H}
+    ch, own, cnt = chains(v, sem)
 
     for k, q in enumerate((sy, s)):
-        q.dma_start(T.sl[16 * k:16 * k + 16, :], T.send[:, :]).then_inc(sem.sld, 16)
-        q.dma_start(T.ul[16 * k:16 * k + 16, :], T.un[:, :]).then_inc(sem.uld, 16)
-    sy.dma_start(T.bsb[:, :], T.b[:, :]).then_inc(sem.bld, 16)
+        q.dma_start(T.su[16 * k:16 * k + 16, 12:24], T.un[:, :]).then_inc(sem.uld, 16)
+        q.dma_start(T.su[16 * k:16 * k + 16, 0:12], T.send[:, :]).then_inc(sem.sld, 16)
+    sy.dma_start(T.pl[0:16, :], T.upl[:, :]).then_inc(sem.pld, 16)
+    sy.dma_start(T.bsb[:, 0:4 * TCOL], T.b[:, :]).then_inc(sem.bld, 16)
     for i in range(4):
         sy.dma_start(T.asb[:, 512 * i:512 * i + 512], T.a[:, 512 * i:512 * i + 512]).then_inc(sem["ald%d" % i], 16)
-    for k in range(2):
-        sy.dma_start(T.pl[16 * k:16 * k + 16, :], T.upl[:, :]).then_inc(sem.pld, 16)
     quarters = [slice(32 * k, 32 * k + 32) for k in range(4)]
 
     g.iota(T.ipm[:, :], [[0, 2]], 0, 1).then_inc(sem.gi, 1)
-    for r in range(0, N, 2):
-        g.iota(T.tab[:, 3 * r:3 * r + 6], [[SLOT[block[r + 1]] - SLOT[block[r]], 2], [0, 3]], SLOT[block[r]], 0).then_inc(sem.gtab, 1)
-    fill(T.cols[:, :], [[1, TCOL]], 0, sem.gcol)
-    fill(T.ramp[:, :], [[1, 516]], -3, sem.gramp, -4)
-    fill(T.val[:, :], [[0, 2], [1, UN]], 0, sem.gval)
-    g.iota(T.ek[:, :], [[16, 6]], 208, 0).then_inc(sem.gval, 1)
-    fill(T.far[:, :], [[1, 288]], UN - OP, sem.gval)
+    g.iota(T.tab[0:32, :], [[0, 2], [d2, 2], [d1 // 2, 3]], first[0], 0).then_inc(sem.gtab, 1)
+    g.iota(T.p16[:, :], [[0, 2]], 0, 16).then_inc(sem.gpick, 1)
+    fill(g, T.hh[:, 0:TCOL], [[1, TCOL]], 0, sem.gcol)
 
-    ch("vl", v.memset(T.row[:, :], float(TCOL)))
-    ch("vz", v.memset(T.zs[:, TCOL:4 * ZW:ZW], 0.0))
+    zeros = [T.bsb[:, 4 * TCOL:4 * BW], T.zs[:, TCOL:4 * ZW:ZW], T.hh[:, TCOL:4 * START]]
+    for out in zeros:
+        v.memset(out, 0.0).then_inc(sem.azero, 1)
     v.wait_ge(sem.gi, 1)
-    ch("vc", v.tensor_scalar(T.h16[:, :], T.ipm[:, :], 16, None, band))
-    ch("vc", v.tensor_scalar(T.h8[:, :], T.ipm[:, :], 8, None, band))
-    ch("vq", v.tensor_scalar(T.q15[:, :], T.ipm[:, :], 15, None, band))
-    for j, n in enumerate(SIZE):
-        if n < 128:
-            ch("vh%d" % j, v.memset(T["h%d" % j][:, 4 * (LEAD[j] + n):4 * (LEAD[j] + 128)], 0.0))
+    for k, m in enumerate((16, 8)):
+        ch("vc", v.tensor_scalar(T.bits[:, k:k + 1], T.ipm[:, 0:1], m, None, band))
+    ch("vq", v.tensor_scalar(T.bits[:, 2:3], T.ipm[:, 0:1], 112, None, band))
     own("vc")
-    ch("vc", v.tensor_scalar(T.sh[:, :], T.h16[:, :], -1, 16, mult, add))
-    ch("vc", v.tensor_scalar(T.up[:, :], T.h8[:, :], -0.125, 1, mult, add))
-    ch("vc", v.tensor_scalar(T.dn[:, :], T.h8[:, :], 0.125, None, mult))
+    ch("vc", v.tensor_scalar(T.col[:, 0:1], T.bits[:, 0:1], -1, 16, mult, add))
+    ch("vc", v.tensor_scalar(T.col[:, 1:2], T.bits[:, 1:2], d1 / 8, -d1 / 2, mult, add))
+    ch("vrowf", v.memset(T.row[:, 0:ROW], float(TCOL)))
+    own("vc")
     own("vq")
-    ch("vi", v.tensor_copy(T.qf[:, :], T.q15[:, :]))
-    own("vc")
-    v.wait_ge(sem.gtab, 4)
-    ch("vc", v.tensor_scalar(T.w1[0:32, :], T.tab[0:32, 0:24:2], T.up[0:32, 0:1], T.sh[0:32, 0:1], mult, add))
-    ch("vc", v.tensor_scalar(T.w2[0:32, :], T.tab[0:32, 1:24:2], T.dn[0:32, 0:1], None, mult))
+    v.wait_ge(sem.gtab, 1)
+    ch("vc", v.tensor_scalar(T.base[0:32, 1:12:3], T.tab[0:32, 1:12:3], T.col[0:32, 0:1], T.col[0:32, 1:2], add, add))
+    for k in (0, 2):
+        ch("vc", v.tensor_scalar(T.base[0:32, k:12:3], T.tab[0:32, k:12:3], T.col[0:32, 0:1], None, add))
+    ch("vq", v.tensor_scalar(T.col[:, 2:3], T.bits[:, 2:3], -16, T.col[:, 0:1], mult, add))
+
+    known = set()
+
+    def once(q, name, val):
+        if (q is s, name) not in known:
+            q.wait_ge(sem[name], val)
+            known.add((q is s, name))
+
+    def into_slots(q, name):
+        j, i = int(name[0]), int(name[1])
+        kind, a, n = TILES[j]
+        once(q, "vlst" + kind, 1)
+        once(q, "azero", len(zeros))
+        once(q, "az%d" % i, 1)
+        c = 16 * (kind == "n")
+        out = T.hh[:, 4 * (END[j] - SPAN[j][1] + SPAN[j][0]) + i:4 * END[j]:4]
+        picked = T.zs[:, ZW * i:ZW * i + TCOL + 1].indirect(T.lst[:, c + SPAN[j][0] // 16:c + SPAN[j][1] // 16])
+        (s.activation(out, picked, copy) if q is s else v.tensor_copy(out, picked)).then_inc(sem["ah%d" % j], 1)
+
+    def quantise(k):
+        n = max(SPAN[k][1] - SLOT[TILES[k][1]], 128)
+        once(v, "gcol", 1)
+        for j in range(k + 1):
+            if END[j] > END[k] - n:
+                once(v, "ah%d" % j, 4)
+        v.quantize_mx(T.hq[:, QW * (k + 1) - n:QW * (k + 1)], T.hs[:, QW * (k + 1) - n:QW * (k + 1)],
+                      T.hh[:, 4 * (END[k] - n):4 * END[k]]).then_inc(sem["vt%d" % k], 1)
 
     def step(name):
+        kind = name[-1]
+        c = ROW * (kind == "n")
         if name[0] == "a":
             i = int(name[1])
             v.wait_ge(sem["ald%d" % i], 16)
             v.quantize_mx(T.aq[:, 128 * i:128 * i + 128], T.asc[:, 128 * i:128 * i + 128],
                           T.asb[:, 512 * i:512 * i + 512]).then_inc(sem["vaq%d" % i], 1)
         elif name == "b":
+            own("vu")
             v.wait_ge(sem.bld, 16)
             v.quantize_mx(T.bq[:, :], T.bs[:, :], T.bsb[:, :]).then_inc(sem.vbq, 1)
-        elif name[0] == "s":
-            v.wait_ge(sem.sld, 32)
-            for q in quarters[2 * int(name[1]):2 * int(name[1]) + 2]:
-                v.tensor_copy(T.osd[q, :], T.sl[0:32, :]).then_inc(sem.vosd, 1)
-        elif name == "base":
-            own("vc")
-            ch("vc", v.tensor_tensor(T.base[0:32, :], T.w1[0:32, :], T.w2[0:32, :], add))
-        elif name == "g":
-            ch("vq", v.tensor_scalar(T.g1[:, :], T.q15[:, :], 16, T.sh[:, 0:1], mult, add))
-        elif name == "pick":
-            own("vq")
-            ch("vp", v.tensor_copy(T.pick[:, 0:1], T.g1[:, 0:1]))
-            ch("vp", v.tensor_scalar(T.pick[:, 1:2], T.g1[:, 1:2], 256, 400, add, AluOpType.min))
         elif name == "un":
             v.wait_ge(sem.uld, 32)
             own("vc")
-            ch("vc", v.tensor_tensor(T.x2[0:32, :], T.ul[0:32, :], T.base[0:32, :], add))
+            ch("vc", v.tensor_tensor(T.su[0:32, 12:24], T.su[0:32, 12:24], T.base[0:32, :], add))
         elif name == "pos":
+            v.wait_ge(sem.sld, 32)
             own("vc")
             for q in quarters:
-                ch("vl", v.tensor_copy(T.pos[q, :], T.x2[0:32, :]))
-        elif name == "row":
-            own("vl")
-            v.wait_ge(sem.avals, 1)
-            ch("vl", v.tensor_copy(T.row[:, :].indirect(T.pos[:, :]), T.vals[:, :]))
-        elif name == "turn":
-            own("vl")
-            ch("vl", v.transpose(T.rowt[:, :], T.row[:, :]))
-        elif name == "list":
+                ch("voff", v.tensor_copy(T.off[q, :], T.su[0:32, :]))
+        elif name == "pick":
+            own("vq")
+            v.wait_ge(sem.gpick, 1)
+            ch("vp", v.tensor_scalar(T.pick[:, :], T.p16[:, :], T.col[:, 2:3], ROW - 16, add, AluOpType.min))
+        elif name == "low":
+            v.wait_ge(sem.pld, 16)
+            ch("vu", v.tensor_scalar(T.pp[0:16, 0:6], T.pl[0:16, :], LOW, None, band))
+        elif name == "high":
+            ch("vw", v.tensor_scalar(T.pp[0:16, 6:12], T.pl[0:16, :], HIGH + 128, None, band))
+        elif name == "parts":
+            once(v, "azero", len(zeros))
+            for k, chain in enumerate(("vu", "vw")):
+                own(chain)
+                ch("vu", v.tensor_copy(T.bsb[0:16, 4 * TCOL + k:4 * BW:4], T.pp[0:16, 6 * k:6 * k + 6]))
+        elif name == "blank":
+            ch("vrown", v.memset(T.row[:, ROW:2 * ROW], float(TCOL)))
+        elif name[:3] == "row":
+            own("vrow" + kind)
+            own("voff")
+            once(v, "azero", len(zeros))
+            v.wait_ge(sem["avals" + kind], 1)
+            k = 6 * half[kind]
+            ch("vrow" + kind, v.tensor_copy(T.row[:, c:c + ROW].indirect(T.off[:, 12 + k:18 + k]), T.vals[:, 16 * k:16 * k + 96]))
+        elif name[:4] == "turn":
+            own("vrow" + kind)
+            ch("vrow" + kind, v.transpose(T.rowt[:, c:c + ROW], T.row[:, c:c + ROW]))
+        elif name[:4] == "list":
             own("vp")
-            own("vl")
-            v.tensor_copy(T.lst[:, :], T.rowt[:, :].indirect(T.pick[:, :])).then_inc(sem.vlst, 1)
+            own("vrow" + kind)
+            k = 16 * (kind == "n")
+            v.tensor_copy(T.lst[:, k:k + 16], T.rowt[:, c:c + ROW].indirect(T.pick[:, 0:1])).then_inc(sem["vlst" + kind], 1)
+        elif name[0] == "q":
+            quantise(int(name[1]))
+        elif name[0] == "z":
+            i = int(name[1])
+            v.wait_ge(sem["tz%d" % i], 1)
+            v.tensor_copy(T.zs[:, ZW * i:ZW * i + TCOL], T["pa%d" % i][:, 0:TCOL]).then_inc(sem["az%d" % i], 1)
+        else:
+            into_slots(v, name)
 
     for name in ORDER:
         step(name)
-    s.wait_ge(sem.gcol, 1)
-    s.wait_ge(sem.vosd, 4)
-    s.activation(T.vals[:, :], T.cols[:, :].indirect(T.osd[:, :]), copy).then_inc(sem.avals, 1)
 
     te.wait_ge(sem.vbq, 1)
     for i in range(4):
         te.wait_ge(sem["vaq%d" % i], 1)
         te.matmul_mx(T["pa%d" % i][:, 0:TCOL], T.aq[:, 128 * i:128 * i + 128], T.asc[:, 128 * i:128 * i + 128],
-                     T.bq[:, :], T.bs[:, :], True, True).then_inc(sem["tz%d" % i], 1)
-
-    def leave(i):
-        s.wait_ge(sem["tz%d" % i], 1)
-        s.activation(T.zs[:, ZW * i:ZW * i + TCOL], T["pa%d" % i][:, 0:TCOL], copy).then_inc(sem["az%d" % i], 1)
-
-    known = {"s": set(), "v": set()}
-
-    def into_slots(who, name):
-        q = s if who == "s" else v
-        i = int(name[1])
-        if i not in known[who]:
-            q.wait_ge(sem["az%d" % i], 1)
-            known[who].add(i)
-        window = T.zs[:, ZW * i:ZW * i + TCOL + 1]
-        if name[0] == "k":
-            s.activation(T.ho[:, 2 * UN * i:2 * UN * (i + 1)], window.indirect(T.lst[:, K3:K3 + 6]), copy).then_inc(sem.ao, 1)
-            return
-        j = int(name[0])
-        out = T["h%d" % j][:, i:4 * (LEAD[j] + SIZE[j]):4]
-        picked = window.indirect(T.lst[:, (FROM[j] - LEAD[j]) // 16:FROM[j + 1] // 16])
-        if who == "s":
-            s.activation(out, picked, copy).then_inc(sem["ah%d" % j], 1)
+                     T.bq[:, 0:TCOL], T.bs[:, 0:TCOL], True, True).then_inc(sem["tz%d" % i], 1)
+    for name in ON_SCALAR:
+        if name[0] == "z":
+            i = int(name[1])
+            s.wait_ge(sem["tz%d" % i], 1)
+            s.activation(T.zs[:, ZW * i:ZW * i + TCOL], T["pa%d" % i][:, 0:TCOL], copy).then_inc(sem["az%d" % i], 1)
+        elif name[0] == "v":
+            k = 6 * half[name[-1]]
+            once(s, "gcol", 1)
+            once(s, "voff", 4)
+            s.activation(T.vals[:, 16 * k:16 * k + 96], T.hh[:, 0:TCOL].indirect(T.off[:, k:k + 6]),
+                         copy).then_inc(sem["avals" + name[-1]], 1)
         else:
-            ch("vh%d" % j, v.tensor_copy(out, picked))
+            into_slots(s, name)
 
-    for i in range(4):
-        leave(i)
-    s.wait_ge(sem.vlst, 1)
-    s.wait_ge(sem.vz, 1)
-    for name in ON_SCALAR + ["k%d" % i for i in range(4)]:
-        into_slots("s", name)
-    v.wait_ge(sem.vlst, 1)
-    own("vz")
-    for name in ON_VECTOR:
-        if name == "cst":
-            v.wait_ge(sem.gramp, 1)
-            ch("vk", v.tensor_scalar(T.cst[:, :], T.ramp[:, :], 0, None, AluOpType.is_equal))
-        elif name == "zero":
-            ch("vg", v.memset(T.hg[:, :], 0.0))
-        elif name[0] == "q":
-            j, n = int(name[1]), sum(x[0] == name[1] for x in ON_SCALAR)
-            if n:
-                v.wait_ge(sem["ah%d" % j], n)
-            own("vh%d" % j)
-            v.quantize_mx(T["hq%d" % j][:, :], T["hs%d" % j][:, :],
-                          T["h%d" % j][:, 4 * LEAD[j]:4 * (LEAD[j] + max(SIZE[j], 128))]).then_inc(sem["vt%d" % j], 1)
+    g.wait_ge(sem.vbq, 1)
+    sent = send(g, T, topo, core, helper[2], ("lq", "ls", 10), ("bq", "bs", TCOL), BW - TCOL, sem.arru, [link, link])
+    for blk in WRITES:
+        j, a = WHERE[blk]
+        g.wait_ge(sem["vt%d" % j], 1)
+        frm = ("hq", "hs", QW * (j + 1) - END[j] + a)
+        if blk in RELAY:
+            sent += send(g, T, topo, core, helper[RELAY.index(blk)], ("rq", "rs", 0), frm, UN, sem.arrr, [rest, rest])
         else:
-            into_slots("v", name)
+            sent += send(g, T, topo, core, peer[int(blk[1])], ("kq", "ks", AT[blk]), frm, UN, sem["arr" + blk])
 
-    sent = 16
-    for i, step in enumerate(PLAN):
-        if TILE.index(TILE[i]) == i:
-            g.wait_ge(sem["vt%d" % TILE[i]], 1)
-        for k in range(2):
-            call = []
-            for j, (n, kinds) in enumerate(step):
-                blk, width, d = (kinds[0], n), UN * len(kinds), peer[n]
-                rid, pid = topo.addr(d, core)
-                e0, count = SHARE[len(step)][k][j]
-                engines = topo.engines(core, d)[k::2] if i < SPLIT else topo.engines(core, d)[e0:e0 + count]
-                src = side(T, "hq%d" % TILE[i], "hs%d" % TILE[i], k, SLOT[blk] - FROM[TILE[i]], width)
-                dst, mask = side(T, "kq", "ks", k, AT[blk], width), sum(1 << e for e in engines)
-                sent += len(engines)
-                if len(step) == 1:
-                    g.remote_dma(dst, src, sem["arr%d" % i], sem.lsend, pid, rid, mask)
-                else:
-                    call.append(RemoteDMATransfer(dst_ids=[DstId(rid=rid, pnc=pid)], dma_engine_mask=mask,
-                                                  remote_sem=sem["arr%d" % i], src=src, dst=dst))
-            if call:
-                g.remote_dma_fused(call, local_sem=sem.lsend)
-
-    def constant(t):
-        a = CONST + 128 * t
-        v.quantize_mx(T.kq[:, a:a + 128], T.ks[:, a:a + 128], T.cst[:, 3 - t:515 - t]).then_inc(sem.veq, 1)
-
-    own("vk")
-    for t in range(4):
-        constant(t)
-    own("vg")
-    v.quantize_mx(T.kq[:, CONST - 128:CONST], T.ks[:, CONST - 128:CONST], T.hg[:, :]).then_inc(sem.veq, 1)
-    v.wait_ge(sem.pld, 32)
-    v.wait_ge(sem.gval, 3)
-    own("vi")
-    gf = topo.host(partner)
-    for q in quarters:
-        ch("vi", v.tensor_scalar(T.p1[q, :], T.pl[0:32, :], 511, None, band))
-    ch("vi", v.tensor_scalar(T.dump[:, :], T.ek[:, :], T.qf[:, 0:1], None, add))
-    ch("vj", v.tensor_scalar(T.inv[:, 0:288], T.far[:, :], T.sh[:, 0:1], UN, AluOpType.subtract, AluOpType.max))
-    own("vi")
-    ch("vi", v.tensor_tensor(T.p2[:, :], T.p1[:, :], T.dump[:, :], AluOpType.min))
-    ch("vz", v.memset(T.sn[:, UN:4 * WIN:WIN], 0.0))
-    ch("vz", v.tensor_copy(T.pu[quarters[3], 0:3], T.pl[0:32, 3 * gf:3 * gf + 3]))
-    own("vi")
-    for h in range(2):
-        ch("vj", v.tensor_scalar(T.po[:, 3 * h:3 * h + 3], T.p2[:, 3 * h:3 * h + 3], T.sh[:, 0:1], OP * (h == gf), add, add))
-    for q in quarters[:3]:
-        ch("vz", v.tensor_copy(T.pu[q, 0:3], T.pl[0:32, 3 * gf:3 * gf + 3]))
-    own("vj")
-    ch("vi", v.tensor_copy(T.inv[:, :].indirect(T.po[:, :]), T.val[:, :]))
-
-    def unpack(bank, step, start, stop, done=None):
-        c = AT[step[0]]
+    def unpack(bank, c, start, stop, done=None):
         for t in range(4):
             a = CONST + 128 * t
             ins = te.matmul_mx(T[bank + str(t)][:, 0:128], T.kq[:, a:a + 128], T.ks[:, a:a + 128],
@@ -311,65 +419,75 @@ def rank_program(g, core, T, topo):
                 ins.then_inc(sem[done + str(t)], 1)
 
     def mine(kind, t):
-        a = 2 * UN * t + SLOT[kind, OWN] - 16 * K3
-        return T.ho[:, a:a + UN]
+        j, a = WHERE[kind + str(OWN)]
+        once(v, "ah%d" % j, 4)
+        return T.hh[:, 4 * a + t:4 * (a + UN):4]
 
-    te.wait_ge(sem.veq, 5)
-    for i in range(3):
-        te.wait_ge(sem["arr%d" % i], 8 if i < SPLIT else 16)
-        unpack("pb", STEPS[i], i == 0, i == 2, "tg" if i == 2 else None)
+    def sums(kind, bank, done):
+        blocks = [blk for blk in LANDS if blk[0] == kind]
+        for blk in blocks:
+            te.wait_ge(sem["arr" + blk], 16)
+            unpack(bank, AT[blk], blk == blocks[0], blk == blocks[-1], done if blk == blocks[-1] else None)
 
-    v.wait_ge(sem.ao, 4)
+    te.wait_ge(sem.arrc, 64)
+    sums("f", "pb", "tg")
+    ch("vq", v.tensor_scalar(T.bits[:, 3:4], T.ipm[:, 0:1], 3, None, band))
+    for t in range(4):
+        ch("vw", v.memset(T.wf[:, YW * t + 2 * UN:YW * (t + 1)], 0.0))
+    own("vq")
+    ch("vw", v.tensor_scalar(T.col[:, 3:4], T.bits[:, 3:4], YW, None, mult))
+
     for t in range(4):
         v.wait_ge(sem["tg%d" % t], 1)
-        ch("vg", v.tensor_tensor(T.hg[:, 320 + t:512:4], T["pb%d" % t][:, 0:UN], mine("f", t), add))
-    own("vi")
-    ch("vi", v.transpose(T.invt[:, :], T.inv[:, 0:288]))
-    own("vg")
-    v.quantize_mx(T.hgq[:, :], T.hgs[:, :], T.hg[:, :]).then_inc(sem.vhg, 1)
-    rid, pid = topo.addr(partner, core)
-    g.wait_ge(sem.vhg, 1)
-    for k in range(2):
-        g.remote_dma(side(T, "kq", "ks", k, AT["p", 0]), side(T, "hgq", "hgs", k, 128 - UN), sem.arrp, sem.lsend,
-                     pid, rid, topo.mask(core, partner))
+        v.tensor_tensor(T.hh[:, 4 * (END[SUM] - UN) + t:4 * END[SUM]:4], T["pb%d" % t][:, 0:UN], mine("f", t),
+                        add).then_inc(sem["ah%d" % SUM], 1)
+    quantise(SUM)
+    g.wait_ge(sem["vt%d" % SUM], 1)
+    sent += send(g, T, topo, core, partner, ("kq", "ks", 0), ("hq", "hs", QW * (SUM + 1) - UN), UN, sem.arrp)
 
-    for t in range(4):
-        ch("vg", v.tensor_tensor(T.xn[:, UN * t:UN * t + UN], T["pb%d" % t][:, UN:2 * UN], mine("n", t), add))
-    own("vi")
-    ch("vz", v.tensor_copy(T.offi[:, :], T.invt[:, :].indirect(T.pick[:, 0:1])))
+    te.wait_ge(sem["ah%d" % SUM], 4)
+    te.wait_ge(sem.arrw, 32)
+    te.wait_ge(sem.arrl, 32)
+    te.matmul_mx(T.pb0[:, 0:128], T.kq[:, TURN:TURN + 128], T.ks[:, TURN:TURN + 128],
+                 T.kq[:, LISTS:LISTS + 128], T.ks[:, LISTS:LISTS + 128], True, True).then_inc(sem.tu, 1)
     for i in range(4):
         te.wait_ge(sem["az%d" % i], 1)
-    te.wait_ge(sem.arr3, 16)
-    unpack("pa", STEPS[3], True, True, "tn")
-    own("vg")
-    def gather(t, need, out, window, done):
-        q = s if t < 2 else v
-        q.wait_ge(sem[need + str(t)], 1)
-        (s.activation(out, window, copy) if t < 2 else v.tensor_copy(out, window)).then_inc(done, 1)
-
+    sums("n", "pa", "tn")
+    own("vw")
+    v.wait_ge(sem.tu, 1)
+    v.tensor_scalar(T.offi[:, 0:24], T.pb0[:, 0:24], T.col[:, 3:4], None, add).then_inc(sem.vinv, 1)
+    v.tensor_copy(T.offi[:, 24:28], T.pb0[:, 24:28]).then_inc(sem.vinv, 1)
     for t in range(4):
         v.wait_ge(sem["tn%d" % t], 1)
-        v.tensor_tensor(T.sn[:, WIN * t:WIN * t + UN], T["pa%d" % t][:, 0:UN], T.xn[:, UN * t:UN * t + UN],
+        v.tensor_tensor(T.wf[:, YW * t + UN:YW * t + 2 * UN], T["pa%d" % t][:, 0:UN], mine("n", t),
                         add).then_inc(sem["vn%d" % t], 1)
-    s.wait_ge(sem.vz, cnt["vz"])
-    own("vz")
+    s.wait_ge(sem.vinv, 2)
+    v.wait_ge(sem.vinv, 2)
+
+    def gather(who, t, need, out, window, done):
+        q = s if who == "s" else v
+        q.wait_ge(sem[need + str(t)], 1)
+        (s.activation(out, window, copy) if who == "s" else v.tensor_copy(out, window)).then_inc(done, 1)
+
     for t in range(4):
-        gather(t, "vn", T.wf[:, YW * t + UN:YW * (t + 1)], T.sn[:, WIN * t:WIN * t + UN + 1].indirect(T.offi[:, 0:6]),
-               sem["ayn%d" % t])
-    for t in range(4):
-        gather(t, "ayn", T.na[:, UN * t:UN * t + UN], T.wf[:, YW * t + UN:YW * (t + 1)].indirect(T.pu[:, 0:3]), sem["an%d" % t])
+        gather("ssvv"[t], t, "vn", T.na[:, UN * t:UN * t + UN],
+               T.wf[:, YW * t + UN:YW * t + 2 * UN + 1].indirect(T.offi[:, 24:27]), sem["an%d" % t])
 
     te.wait_ge(sem.arrp, 16)
-    te.wait_ge(sem.vg, cnt["vg"])
-    unpack("pb", [("p", 0)], True, True, "tl")
+    te.wait_ge(sem.vinv, 2)
+    unpack("pb", 0, True, True, "tl")
     for t in range(4):
         v.wait_ge(sem["an%d" % t], 1)
         v.wait_ge(sem["tl%d" % t], 1)
         v.tensor_tensor(T.wf[:, YW * t:YW * t + UN], T["pb%d" % t][:, 0:UN], T.na[:, UN * t:UN * t + UN],
-                        add).then_inc(sem["am%d" % t], 1)
-    for t in range(4):
-        gather(t, "am", T.yo[:, t:4 * OP:4], T.wf[:, YW * t:YW * (t + 1)].indirect(T.offi[:, 6:12]), sem.vy)
-    sy.wait_ge(sem.vy, 4)
-    sy.dma_start(T.y[:, :], T.yo[:, 0:4 * OC]).then_inc(sem.yst, 16)
-    sy.wait_ge(sem.yst, 16)
+                        add).then_inc(sem.am0, 1)
+    s.wait_ge(sem.am0, 4)
+    v.wait_ge(sem.am0, 4)
+    for k, (a, b, c) in enumerate(LAST):
+        s.activation(T.yo[:, 16 * a:16 * b], T.wf[:, :].indirect(T.offi[:, a:b]), copy).then_inc(sem["ay%d" % k], 1)
+        v.tensor_copy(T.yo[:, 16 * b:16 * c], T.wf[:, :].indirect(T.offi[:, b:c])).then_inc(sem["ay%d" % k], 1)
+        q = sy
+        q.wait_ge(sem["ay%d" % k], 2)
+        q.dma_start(T.y[:, 16 * a:16 * c], T.yo[:, 16 * a:16 * c]).then_inc(sem.yst, 16)
+    sy.wait_ge(sem.yst, 16 * len(LAST))
     g.wait_ge(sem.lsend, sent)

from concourse.mybir import dt, AluOpType, ActivationFunctionType

N, TCOL, CAPP, OC, UN = 8, 192, 24, 88, 48
H = 4
OWN = H - 1
ZW = 208
SLOT = [0, 64, 112, 176]
ROW = 256
OP = 96
YW = 104
IW = 144
LOW, HIGH = 7, 120
BW = TCOL + 6

TILES = [("f", 0, 1), ("f", 1, 2), ("n", 0, 1), ("n", 1, 2), ("f", 3, 1), ("s", 0, 1), ("n", 3, 1)]
WRITES = ["f0", "f1", "f2", "n0", "n1", "n2"]
RELAY = []
LANDS = ["f0", "f1", "f2", "n0", "n1", "n2"]

ORDER = "un pick pos low high blank parts b a0 rowf a1 a2 turnf a3 listf 00 z3 03 q0 rown 13 turnn q1 listn 22 23 q2 32 33 q3 42 43".split()
ON_SCALAR = "valf valn z0 z1 z2 02 01 10 11 12 20 21 30 31 40 41 60 61 62 63".split()
LAST = [(0, 6, 12), (12, 16, 22)]


def layout():
    span = [(SLOT[a] // 32 * 32, SLOT[a + n - 1] + UN) for kind, a, n in TILES]
    start = max(TCOL // 4, 128 - span[0][1] + span[0][0])
    end, at = [], start
    for a, b in span:
        at += b - a
        end.append(at)
    where = {kind + str(i): (j, end[j] - span[j][1] + SLOT[i]) for j, (kind, a, n) in enumerate(TILES) for i in range(a, a + n)}
    return span, start, end, where


SPAN, START, END, WHERE = layout()
SUM = WHERE["s0"][0]
QW = 192
AT = {blk: UN * (len(LANDS) - i) for i, blk in enumerate(LANDS)}
CONST = UN * (len(LANDS) + 1)
LISTS = CONST + 512
TURN = LISTS + 28

F32, BF, I32, U16 = "float32", "bfloat16", "int32", "uint16"
CODE, PLANE = "float8_e4m3fn_x4", "uint8"
SCRATCH = {
    "asb": ("sbuf", [128, 2048], BF), "bsb": ("sbuf", [128, 4 * BW], BF),
    "su": ("sbuf", [128, 24], I32), "pl": ("sbuf", [128, 6], I32), "pp": ("sbuf", [128, 12], I32),
    "ipm": ("sbuf", [128, 2], I32), "p16": ("sbuf", [128, 2], I32), "bits": ("sbuf", [128, 8], I32), "col": ("sbuf", [128, 8], F32),
    "tab": ("sbuf", [128, 12], I32), "base": ("sbuf", [128, 12], I32),
    "off": ("sbuf", [128, 24], U16), "pick": ("sbuf", [128, 2], U16), "lst": ("sbuf", [128, 32], U16),
    "offi": ("sbuf", [128, 28], U16), "vals": ("sbuf", [128, TCOL], BF),
    "row": ("sbuf", [128, 2 * ROW], BF), "rowt": ("sbuf", [128, 2 * ROW], BF),
    "aq": ("sbuf", [128, 512], CODE), "asc": ("sbuf", [128, 512], PLANE),
    "bq": ("sbuf", [128, BW], CODE), "bs": ("sbuf", [128, BW], PLANE),
    "zs": ("sbuf", [128, 4 * ZW], BF), "hh": ("sbuf", [128, 4 * END[-1]], BF),
    "hq": ("sbuf", [128, QW * len(TILES)], CODE), "hs": ("sbuf", [128, QW * len(TILES)], PLANE),
    "kq": ("sbuf", [128, TURN + 128], CODE), "ks": ("sbuf", [128, TURN + 128], PLANE),
    "wf": ("sbuf", [128, 4 * YW], F32), "na": ("sbuf", [128, 4 * UN], F32), "yo": ("sbuf", [128, 4 * OP], F32),
    "ones": ("sbuf", [128, 516], BF), "ramp": ("sbuf", [128, 516], BF), "cst": ("sbuf", [128, 516], BF),
    "first": ("sbuf", [128, 2], F32), "cq": ("sbuf", [128, 256], CODE), "cs": ("sbuf", [128, 256], PLANE),
    "rq": ("sbuf", [128, UN], CODE), "rs": ("sbuf", [128, UN], PLANE),
    "lq": ("sbuf", [128, 144], CODE), "ls": ("sbuf", [128, 144], PLANE),
    "w16": ("sbuf", [128, 128], BF), "w4": ("sbuf", [128, 32], BF), "wl": ("sbuf", [128, 512], BF), "wr": ("sbuf", [128, 512], BF),
    "dump": ("sbuf", [128, 6], F32), "ek": ("sbuf", [128, 6], F32), "place2": ("sbuf", [128, 6], F32),
    "po": ("sbuf", [128, 10], U16), "cg": ("sbuf", [128, 8], U16), "e16": ("sbuf", [128, 6], F32), "val": ("sbuf", [128, 2 * UN], BF),
    "inv": ("sbuf", [128, 2 * IW], BF), "lrow": ("sbuf", [128, 192], BF),
    "li": ("sbuf", [128, 112], I32), "lj": ("sbuf", [128, 112], I32), "lt": ("sbuf", [128, 512], BF),
}
for _i in range(4):
    SCRATCH["pa%d" % _i] = ("psum", [128, 512], F32)
    SCRATCH["pb%d" % _i] = ("psum", [128, 512], F32)

SEMAPHORES = (["sld", "uld", "pld", "bld", "yst", "lsend", "gi", "gtab", "gcol", "gval", "gpick", "azero", "apart",
               "vc", "vq", "vp", "vl", "vi", "vj", "vk", "vu", "vw", "voff", "vbq", "vg", "vhg", "vy",
               "arrp", "arrc", "arrw", "arrl", "arru", "arrr", "tu", "vinv"]
              + [p + k for p in ("avals", "vrow", "vlst") for k in "fn"] + ["arr" + blk for blk in LANDS]
              + [p + str(i) for p in ("ald", "vaq", "tz", "az", "tg", "tn", "tl", "am", "an", "vn", "ay") for i in range(4)]
              + [p + str(i) for p in ("ah", "vt") for i in range(len(TILES))])


def turn(topo, dst, src):
    if dst == src:
        return OWN
    if topo.mates(dst, src):
        return 2
    return 1 if topo.same_plane(dst, src) else 0


def peers(T, topo, core):
    return {turn(topo, c, core): c for c in T.cores if topo.host(c) == topo.host(core)}


def neighbours(T, topo, home):
    idle = [c for c in topo.cores_of(home) if c != home and topo.die(c) == topo.die(home)]
    jobs = []
    for blk in RELAY:
        jobs.append([c for c in idle if c not in jobs and topo.may_write(c, peers(T, topo, home)[int(blk[1])])][0])
    return jobs + [c for c in idle if c not in jobs]


def side(T, q, p, k, a, n):
    return T[p][:, a:a + n] if k else T[q][:, a:a + n].bitcast(dt.uint8)


def send(g, T, topo, core, dst, to, frm, n, arrival, engines=None):
    rid, pid = topo.addr(dst, core)
    engines = engines or [topo.engines(core, dst)] * 2
    for k in range(2):
        g.remote_dma(side(T, to[0], to[1], k, to[2], n), side(T, frm[0], frm[1], k, frm[2], n), arrival, T.sem.lsend,
                     pid, rid, sum(1 << e for e in engines[k]))
    return len(engines[0]) + len(engines[1])


def chains(v, sem):
    cnt = {}

    def ch(name, ins):
        ins.then_inc(sem[name], 1)
        cnt[name] = cnt.get(name, 0) + 1

    def own(name):
        v.wait_ge(sem[name], cnt[name])

    return ch, own, cnt


def fill(g, out, pattern, base, done, step=0):
    g.iota(out, pattern, base, step, allow_small_or_imprecise_dtypes=True).then_inc(done, 1)


def constants_program(g, core, T, topo, home, half):
    v, sem = g.vector, T.sem
    ch, own, cnt = chains(v, sem)
    fill(g, T.first[:, :], [[0, 2]], -4, sem.gi, -4)
    ch("vc", v.memset(T.ones[:, :], 1.0))
    own("vc")
    v.wait_ge(sem.gi, 1)
    ch("vc", v.tensor_tensor_scan(T.ramp[:, :], T.ones[:, :], T.ones[:, :], T.first[:, 0:1], AluOpType.add, AluOpType.mult))
    own("vc")
    ch("vc", v.tensor_scalar(T.cst[:, :], T.ramp[:, :], 0, None, AluOpType.is_equal))
    own("vc")
    for k in range(2):
        t, a = 2 * half + k, 128 * k
        ch("vk", v.quantize_mx(T.cq[:, a:a + 128], T.cs[:, a:a + 128], T.cst[:, 3 - t:515 - t]))
    g.wait_ge(sem.vk, cnt["vk"])
    sent = send(g, T, topo, core, home, ("kq", "ks", CONST + 256 * half), ("cq", "cs", 0), 256, sem.arrc)
    if half < len(RELAY):
        blk = RELAY[half]
        g.wait_ge(sem.arrr, 16)
        sent += send(g, T, topo, core, peers(T, topo, home)[int(blk[1])], ("kq", "ks", AT[blk]), ("rq", "rs", 0), UN, sem["arr" + blk])
    g.wait_ge(sem.lsend, sent)


def lists_program(g, core, T, topo, home, far):
    v, te, sem = g.vector, g.tensor, T.sem
    add, mult, band, low = AluOpType.add, AluOpType.mult, AluOpType.bitwise_and, AluOpType.min
    ch, own, cnt = chains(v, sem)
    g.iota(T.ipm[:, :], [[0, 2]], 0, 1).then_inc(sem.gi, 1)
    fill(g, T.w4[:, :], [[0, 8], [16, 4]], 0, sem.gtab, -1)
    fill(g, T.w16[:, :], [[0, 8], [1, 16]], 0, sem.gcol, -1)
    fill(g, T.ek[:, :], [[0, 2], [16, 3]], OC, sem.gval)
    fill(g, T.e16[:, :], [[16, 6]], 0, sem.gval)
    fill(g, T.val[:, :], [[UN * (1 - 2 * far), 2], [1, UN]], UN * far, sem.gval)
    ch("vw", v.memset(T.wr[:, :], 0.0))
    ch("vl", v.memset(T.wl[:, :], 0.0))
    v.wait_ge(sem.gi, 1)
    for k, m in enumerate((15, 12, 3, 48, 64)):
        ch("vc", v.tensor_scalar(T.bits[:, k:k + 1], T.ipm[:, 0:1], m, None, band))
    own("vc")
    ch("vw", v.tensor_scalar(T.col[:, 6:7], T.bits[:, 4:5], -1, None, mult))
    own("vw")
    v.wait_ge(sem.gtab, 1)
    for t in range(4):
        ch("vw", v.tensor_scalar(T.wr[:, 5 * t:512:16], T.w4[:, :], T.col[:, 6:7], None, AluOpType.is_equal))
    own("vw")
    v.quantize_mx(T.cq[:, 0:128], T.cs[:, 0:128], T.wr[:, :]).then_inc(sem.vk, 1)
    g.wait_ge(sem.vk, 1)
    sent = send(g, T, topo, core, home, ("kq", "ks", TURN), ("cq", "cs", 0), 128, sem.arrw)
    own("vl")
    v.wait_ge(sem.gcol, 1)
    for t in range(2):
        ch("vl", v.tensor_scalar(T.wl[:, t:512:4], T.w16[:, :], 0, None, AluOpType.is_equal))
    own("vc")
    ch("vc", v.tensor_copy(T.col[:, 0:4], T.bits[:, 0:4]))
    ch("vi", v.memset(T.inv[:, :], float(2 * UN)))
    ch("vj", v.memset(T.lrow[:, :], 0.0))
    ch("vu", v.memset(T.lt[:, :], 0.0))
    own("vl")
    v.quantize_mx(T.lq[:, 16:144], T.ls[:, 16:144], T.wl[:, :]).then_inc(sem.vq, 1)
    own("vc")
    v.wait_ge(sem.gval, 3)
    ch("vc", v.tensor_scalar(T.dump[:, :], T.ek[:, :], T.col[:, 0:1], None, add))
    ch("vc", v.tensor_scalar(T.col[:, 4:5], T.col[:, 1:2], 4, T.col[:, 2:3], mult, add))
    ch("vc", v.tensor_scalar(T.col[:, 7:8], T.col[:, 3:4], 1 / 16, T.col[:, 1:2], mult, add))
    own("vc")
    ch("vc", v.tensor_scalar(T.col[:, 5:6], T.col[:, 3:4], 0.25, T.col[:, 4:5], mult, add))
    own("vc")
    ch("vp", v.tensor_scalar(T.cg[:, 0:6], T.e16[:, :], T.col[:, 7:8], None, add))
    ch("vp", v.tensor_scalar(T.cg[:, 6:7], T.col[:, 5:6], OP, None, add))

    te.wait_ge(sem.vq, 1)
    te.wait_ge(sem.arru, 16)
    te.matmul_mx(T.pa0[:, 0:128], T.lq[:, 16:144], T.ls[:, 16:144], T.lq[:, 10:138], T.ls[:, 10:138], True, True).then_inc(sem.tu, 1)
    v.wait_ge(sem.tu, 1)
    ch("vc", v.tensor_tensor(T.place2[:, :], T.pa0[:, 0:6], T.dump[:, :], low))
    own("vc")
    for h in range(2):
        ch("vi", v.tensor_scalar(T.po[:, 3 * h:3 * h + 3], T.place2[:, 3 * h:3 * h + 3], IW * (h == far), None, add))
    ch("vi", v.tensor_copy(T.po[:, 6:9], T.place2[:, 3 * far:3 * far + 3]))
    own("vi")
    ch("vi", v.tensor_copy(T.inv[:, :].indirect(T.po[:, 0:6]), T.val[:, :]))
    own("vi")
    own("vj")
    ch("vj", v.tensor_tensor(T.lrow[:, 0:OP], T.inv[:, 0:OP], T.inv[:, IW:IW + OP], low))
    ch("vj", v.tensor_scalar(T.lrow[:, OP:OP + UN], T.inv[:, 0:IW].indirect(T.po[:, 6:9]), -UN, None, add))
    own("vj")
    own("vp")
    ch("vj", v.tensor_copy(T.li[:, :], T.lrow[:, :].indirect(T.cg[:, 0:7])))
    own("vj")
    for h, m in enumerate((LOW, HIGH)):
        ch("vj", v.tensor_scalar(T.lj[64 * h:64 * h + 64, :], T.li[64 * h:64 * h + 64, :], m, None, band))
    own("vj")
    own("vu")
    ch("vu", v.tensor_copy(T.lt[:, 0:112], T.lj[:, :]))
    own("vu")
    v.quantize_mx(T.cq[:, 128:256], T.cs[:, 128:256], T.lt[:, :]).then_inc(sem.vk, 1)
    g.wait_ge(sem.vk, 2)
    sent += send(g, T, topo, core, home, ("kq", "ks", LISTS), ("cq", "cs", 128), TURN - LISTS, sem.arrl)
    g.wait_ge(sem.lsend, sent)


def rank_program(g, core, T, topo):
    rank = T.rank_of(core)
    if rank is None:
        for home in T.cores:
            if core in neighbours(T, topo, home):
                job = neighbours(T, topo, home).index(core)
                if job < 2:
                    constants_program(g, core, T, topo, home, job)
                else:
                    lists_program(g, core, T, topo, home, 1 - topo.host(home))
        return
    v, s, te, sy, sem = g.vector, g.scalar, g.tensor, g.sync, T.sem
    add, mult, band = AluOpType.add, AluOpType.mult, AluOpType.bitwise_and
    copy = ActivationFunctionType.Copy
    here = [r for r in range(N) if topo.host(T.cores[r]) == topo.host(core)]
    there = [r for r in range(N) if topo.host(T.cores[r]) != topo.host(core)]
    peer, helper = peers(T, topo, core), neighbours(T, topo, core)
    partner = T.cores[there[here.index(rank)]]
    link = topo.engines(core, partner)
    rest = [e for e in topo.engines(core, helper[0]) if e not in link]
    first = [SLOT[turn(topo, T.cores[r], core)] for r in here]
    d1, d2 = first[1] - first[0], first[2] - first[0]
    assert first[3] == first[0] + d1 + d2
    half = {"f": there[0] // H, "n": here[0] // H}
    ch, own, cnt = chains(v, sem)

    for k, q in enumerate((sy, s)):
        q.dma_start(T.su[16 * k:16 * k + 16, 12:24], T.un[:, :]).then_inc(sem.uld, 16)
        q.dma_start(T.su[16 * k:16 * k + 16, 0:12], T.send[:, :]).then_inc(sem.sld, 16)
    sy.dma_start(T.pl[0:16, :], T.upl[:, :]).then_inc(sem.pld, 16)
    sy.dma_start(T.bsb[:, 0:4 * TCOL], T.b[:, :]).then_inc(sem.bld, 16)
    for i in range(4):
        sy.dma_start(T.asb[:, 512 * i:512 * i + 512], T.a[:, 512 * i:512 * i + 512]).then_inc(sem["ald%d" % i], 16)
    quarters = [slice(32 * k, 32 * k + 32) for k in range(4)]

    g.iota(T.ipm[:, :], [[0, 2]], 0, 1).then_inc(sem.gi, 1)
    g.iota(T.tab[0:32, :], [[0, 2], [d2, 2], [d1 // 2, 3]], first[0], 0).then_inc(sem.gtab, 1)
    g.iota(T.p16[:, :], [[0, 2]], 0, 16).then_inc(sem.gpick, 1)
    fill(g, T.hh[:, 0:TCOL], [[1, TCOL]], 0, sem.gcol)

    zeros = [T.bsb[:, 4 * TCOL:4 * BW], T.zs[:, TCOL:4 * ZW:ZW], T.hh[:, TCOL:4 * START]]
    for out in zeros:
        v.memset(out, 0.0).then_inc(sem.azero, 1)
    v.wait_ge(sem.gi, 1)
    for k, m in enumerate((16, 8)):
        ch("vc", v.tensor_scalar(T.bits[:, k:k + 1], T.ipm[:, 0:1], m, None, band))
    ch("vq", v.tensor_scalar(T.bits[:, 2:3], T.ipm[:, 0:1], 112, None, band))
    own("vc")
    ch("vc", v.tensor_scalar(T.col[:, 0:1], T.bits[:, 0:1], -1, 16, mult, add))
    ch("vc", v.tensor_scalar(T.col[:, 1:2], T.bits[:, 1:2], d1 / 8, -d1 / 2, mult, add))
    ch("vrowf", v.memset(T.row[:, 0:ROW], float(TCOL)))
    own("vc")
    own("vq")
    v.wait_ge(sem.gtab, 1)
    ch("vc", v.tensor_scalar(T.base[0:32, 1:12:3], T.tab[0:32, 1:12:3], T.col[0:32, 0:1], T.col[0:32, 1:2], add, add))
    for k in (0, 2):
        ch("vc", v.tensor_scalar(T.base[0:32, k:12:3], T.tab[0:32, k:12:3], T.col[0:32, 0:1], None, add))
    ch("vq", v.tensor_scalar(T.col[:, 2:3], T.bits[:, 2:3], -16, T.col[:, 0:1], mult, add))

    known = set()

    def once(q, name, val):
        if (q is s, name) not in known:
            q.wait_ge(sem[name], val)
            known.add((q is s, name))

    def into_slots(q, name):
        j, i = int(name[0]), int(name[1])
        kind, a, n = TILES[j]
        once(q, "vlst" + kind, 1)
        once(q, "azero", len(zeros))
        once(q, "az%d" % i, 1)
        c = 16 * (kind == "n")
        out = T.hh[:, 4 * (END[j] - SPAN[j][1] + SPAN[j][0]) + i:4 * END[j]:4]
        picked = T.zs[:, ZW * i:ZW * i + TCOL + 1].indirect(T.lst[:, c + SPAN[j][0] // 16:c + SPAN[j][1] // 16])
        (s.activation(out, picked, copy) if q is s else v.tensor_copy(out, picked)).then_inc(sem["ah%d" % j], 1)

    def quantise(k):
        n = max(SPAN[k][1] - SLOT[TILES[k][1]], 128)
        once(v, "gcol", 1)
        for j in range(k + 1):
            if END[j] > END[k] - n:
                once(v, "ah%d" % j, 4)
        v.quantize_mx(T.hq[:, QW * (k + 1) - n:QW * (k + 1)], T.hs[:, QW * (k + 1) - n:QW * (k + 1)],
                      T.hh[:, 4 * (END[k] - n):4 * END[k]]).then_inc(sem["vt%d" % k], 1)

    def step(name):
        kind = name[-1]
        c = ROW * (kind == "n")
        if name[0] == "a":
            i = int(name[1])
            v.wait_ge(sem["ald%d" % i], 16)
            v.quantize_mx(T.aq[:, 128 * i:128 * i + 128], T.asc[:, 128 * i:128 * i + 128],
                          T.asb[:, 512 * i:512 * i + 512]).then_inc(sem["vaq%d" % i], 1)
        elif name == "b":
            own("vu")
            v.wait_ge(sem.bld, 16)
            v.quantize_mx(T.bq[:, :], T.bs[:, :], T.bsb[:, :]).then_inc(sem.vbq, 1)
        elif name == "un":
            v.wait_ge(sem.uld, 32)
            own("vc")
            ch("vc", v.tensor_tensor(T.su[0:32, 12:24], T.su[0:32, 12:24], T.base[0:32, :], add))
        elif name == "pos":
            v.wait_ge(sem.sld, 32)
            own("vc")
            for q in quarters:
                ch("voff", v.tensor_copy(T.off[q, :], T.su[0:32, :]))
        elif name == "pick":
            own("vq")
            v.wait_ge(sem.gpick, 1)
            ch("vp", v.tensor_scalar(T.pick[:, :], T.p16[:, :], T.col[:, 2:3], ROW - 16, add, AluOpType.min))
        elif name == "low":
            v.wait_ge(sem.pld, 16)
            ch("vu", v.tensor_scalar(T.pp[0:16, 0:6], T.pl[0:16, :], LOW, None, band))
        elif name == "high":
            ch("vw", v.tensor_scalar(T.pp[0:16, 6:12], T.pl[0:16, :], HIGH + 128, None, band))
        elif name == "parts":
            once(v, "azero", len(zeros))
            for k, chain in enumerate(("vu", "vw")):
                own(chain)
                ch("vu", v.tensor_copy(T.bsb[0:16, 4 * TCOL + k:4 * BW:4], T.pp[0:16, 6 * k:6 * k + 6]))
        elif name == "blank":
            ch("vrown", v.memset(T.row[:, ROW:2 * ROW], float(TCOL)))
        elif name[:3] == "row":
            own("vrow" + kind)
            own("voff")
            once(v, "azero", len(zeros))
            v.wait_ge(sem["avals" + kind], 1)
            k = 6 * half[kind]
            ch("vrow" + kind, v.tensor_copy(T.row[:, c:c + ROW].indirect(T.off[:, 12 + k:18 + k]), T.vals[:, 16 * k:16 * k + 96]))
        elif name[:4] == "turn":
            own("vrow" + kind)
            ch("vrow" + kind, v.transpose(T.rowt[:, c:c + ROW], T.row[:, c:c + ROW]))
        elif name[:4] == "list":
            own("vp")
            own("vrow" + kind)
            k = 16 * (kind == "n")
            v.tensor_copy(T.lst[:, k:k + 16], T.rowt[:, c:c + ROW].indirect(T.pick[:, 0:1])).then_inc(sem["vlst" + kind], 1)
        elif name[0] == "q":
            quantise(int(name[1]))
        elif name[0] == "z":
            i = int(name[1])
            v.wait_ge(sem["tz%d" % i], 1)
            v.tensor_copy(T.zs[:, ZW * i:ZW * i + TCOL], T["pa%d" % i][:, 0:TCOL]).then_inc(sem["az%d" % i], 1)
        else:
            into_slots(v, name)

    for name in ORDER:
        step(name)

    te.wait_ge(sem.vbq, 1)
    for i in range(4):
        te.wait_ge(sem["vaq%d" % i], 1)
        te.matmul_mx(T["pa%d" % i][:, 0:TCOL], T.aq[:, 128 * i:128 * i + 128], T.asc[:, 128 * i:128 * i + 128],
                     T.bq[:, 0:TCOL], T.bs[:, 0:TCOL], True, True).then_inc(sem["tz%d" % i], 1)
    for name in ON_SCALAR:
        if name[0] == "z":
            i = int(name[1])
            s.wait_ge(sem["tz%d" % i], 1)
            s.activation(T.zs[:, ZW * i:ZW * i + TCOL], T["pa%d" % i][:, 0:TCOL], copy).then_inc(sem["az%d" % i], 1)
        elif name[0] == "v":
            k = 6 * half[name[-1]]
            once(s, "gcol", 1)
            once(s, "voff", 4)
            s.activation(T.vals[:, 16 * k:16 * k + 96], T.hh[:, 0:TCOL].indirect(T.off[:, k:k + 6]),
                         copy).then_inc(sem["avals" + name[-1]], 1)
        else:
            into_slots(s, name)

    g.wait_ge(sem.vbq, 1)
    sent = send(g, T, topo, core, helper[2], ("lq", "ls", 10), ("bq", "bs", TCOL), BW - TCOL, sem.arru, [link, link])
    for blk in WRITES:
        j, a = WHERE[blk]
        g.wait_ge(sem["vt%d" % j], 1)
        frm = ("hq", "hs", QW * (j + 1) - END[j] + a)
        if blk in RELAY:
            sent += send(g, T, topo, core, helper[RELAY.index(blk)], ("rq", "rs", 0), frm, UN, sem.arrr, [rest, rest])
        else:
            sent += send(g, T, topo, core, peer[int(blk[1])], ("kq", "ks", AT[blk]), frm, UN, sem["arr" + blk])

    def unpack(bank, c, start, stop, done=None):
        for t in range(4):
            a = CONST + 128 * t
            ins = te.matmul_mx(T[bank + str(t)][:, 0:128], T.kq[:, a:a + 128], T.ks[:, a:a + 128],
                               T.kq[:, c:c + 128], T.ks[:, c:c + 128], start, stop)
            if done:
                ins.then_inc(sem[done + str(t)], 1)

    def mine(kind, t):
        j, a = WHERE[kind + str(OWN)]
        once(v, "ah%d" % j, 4)
        return T.hh[:, 4 * a + t:4 * (a + UN):4]

    def sums(kind, bank, done):
        blocks = [blk for blk in LANDS if blk[0] == kind]
        for blk in blocks:
            te.wait_ge(sem["arr" + blk], 16)
            unpack(bank, AT[blk], blk == blocks[0], blk == blocks[-1], done if blk == blocks[-1] else None)

    te.wait_ge(sem.arrc, 64)
    sums("f", "pb", "tg")
    ch("vq", v.tensor_scalar(T.bits[:, 3:4], T.ipm[:, 0:1], 3, None, band))
    for t in range(4):
        ch("vw", v.memset(T.wf[:, YW * t + 2 * UN:YW * (t + 1)], 0.0))
    own("vq")
    ch("vw", v.tensor_scalar(T.col[:, 3:4], T.bits[:, 3:4], YW, None, mult))

    for t in range(4):
        v.wait_ge(sem["tg%d" % t], 1)
        v.tensor_tensor(T.hh[:, 4 * (END[SUM] - UN) + t:4 * END[SUM]:4], T["pb%d" % t][:, 0:UN], mine("f", t),
                        add).then_inc(sem["ah%d" % SUM], 1)
    quantise(SUM)
    g.wait_ge(sem["vt%d" % SUM], 1)
    sent += send(g, T, topo, core, partner, ("kq", "ks", 0), ("hq", "hs", QW * (SUM + 1) - UN), UN, sem.arrp)

    te.wait_ge(sem["ah%d" % SUM], 4)
    te.wait_ge(sem.arrw, 32)
    te.wait_ge(sem.arrl, 32)
    te.matmul_mx(T.pb0[:, 0:128], T.kq[:, TURN:TURN + 128], T.ks[:, TURN:TURN + 128],
                 T.kq[:, LISTS:LISTS + 128], T.ks[:, LISTS:LISTS + 128], True, True).then_inc(sem.tu, 1)
    for i in range(4):
        te.wait_ge(sem["az%d" % i], 1)
    sums("n", "pa", "tn")
    own("vw")
    v.wait_ge(sem.tu, 1)
    v.tensor_scalar(T.offi[:, 0:24], T.pb0[:, 0:24], T.col[:, 3:4], None, add).then_inc(sem.vinv, 1)
    v.tensor_copy(T.offi[:, 24:28], T.pb0[:, 24:28]).then_inc(sem.vinv, 1)
    for t in range(4):
        v.wait_ge(sem["tn%d" % t], 1)
        v.tensor_tensor(T.wf[:, YW * t + UN:YW * t + 2 * UN], T["pa%d" % t][:, 0:UN], mine("n", t),
                        add).then_inc(sem["vn%d" % t], 1)
    s.wait_ge(sem.vinv, 2)
    v.wait_ge(sem.vinv, 2)

    def gather(who, t, need, out, window, done):
        q = s if who == "s" else v
        q.wait_ge(sem[need + str(t)], 1)
        (s.activation(out, window, copy) if who == "s" else v.tensor_copy(out, window)).then_inc(done, 1)

    for t in range(4):
        gather("ssvv"[t], t, "vn", T.na[:, UN * t:UN * t + UN],
               T.wf[:, YW * t + UN:YW * t + 2 * UN + 1].indirect(T.offi[:, 24:27]), sem["an%d" % t])

    te.wait_ge(sem.arrp, 16)
    te.wait_ge(sem.vinv, 2)
    unpack("pb", 0, True, True, "tl")
    for t in range(4):
        v.wait_ge(sem["an%d" % t], 1)
        v.wait_ge(sem["tl%d" % t], 1)
        v.tensor_tensor(T.wf[:, YW * t:YW * t + UN], T["pb%d" % t][:, 0:UN], T.na[:, UN * t:UN * t + UN],
                        add).then_inc(sem.am0, 1)
    s.wait_ge(sem.am0, 4)
    v.wait_ge(sem.am0, 4)
    for k, (a, b, c) in enumerate(LAST):
        s.activation(T.yo[:, 16 * a:16 * b], T.wf[:, :].indirect(T.offi[:, a:b]), copy).then_inc(sem["ay%d" % k], 1)
        v.tensor_copy(T.yo[:, 16 * b:16 * c], T.wf[:, :].indirect(T.offi[:, b:c])).then_inc(sem["ay%d" % k], 1)
        q = sy
        q.wait_ge(sem["ay%d" % k], 2)
        q.dma_start(T.y[:, 16 * a:16 * c], T.yo[:, 16 * a:16 * c]).then_inc(sem.yst, 16)
    sy.wait_ge(sem.yst, 16 * len(LAST))
    g.wait_ge(sem.lsend, sent)
